import numpy as np
import ml_dtypes


def mxq(x, axis, fmt="e4m3"):
    dtype, down = {"e4m3": (ml_dtypes.float8_e4m3fn, 7), "e5m2": (ml_dtypes.float8_e5m2, 14)}[fmt]
    v = np.moveaxis(np.asarray(x, np.float32).astype(ml_dtypes.bfloat16).astype(np.float64), axis, -1)
    blocks = v.reshape(v.shape[:-1] + (-1, 32))
    amax = np.abs(blocks).max(-1, keepdims=True)
    byte = np.maximum(np.where(amax > 0, np.frexp(amax)[1] - 1 + 127, 0) - down, 1)
    scale = np.exp2(byte - 127.0)
    codes = (blocks / scale).astype(np.float32).astype(dtype).astype(np.float64)
    return np.moveaxis((codes * scale).reshape(v.shape), -1, axis)


WIDE = False


def mx_kscale(k):
    if not WIDE:
        return np.ones(k)
    levels = np.array([10, -10, 5, -5, 0])
    if k % 512:
        return np.exp2(np.random.permutation(np.resize(levels, k // 32))).repeat(32)
    a = np.empty((k // 512, 16))
    for p in range(k // 512):
        a[p, :8] = np.random.permutation(np.resize(levels, 8))
        for g in range(8):
            far = levels[np.abs(levels - a[p, g]) >= 10]
            a[p, g + 8] = far[np.random.randint(len(far))]
    return np.exp2(a.ravel()).repeat(32)


def f64(x):
    return np.asarray(x).astype(np.float64)


def striped(idx):
    return np.tile(idx.reshape(-1, 16).T, (8, 1)).astype(np.uint16)


def unstriped(offs):
    return offs[:16].T.reshape(-1).astype(np.int64)


def relu(v):
    return np.maximum(v, 0.0)


K, T, S, V, H, N = 512, 1024, 512, 1024, 512, 128
P = 2 ** 7


def setup_inputs():
    n = np.random.standard_normal
    s = mx_kscale(K)[:, None]
    u = mx_kscale(H)
    return {
        "xT": (n((K, T)) * s).astype(np.float32),
        "w1": (n((K, H)) / np.sqrt(K) / s * u).astype(np.float32),
        "w2": (n((H, N)) / np.sqrt(H) / u[:, None]).astype(np.float32),
        "gate": np.tile(np.random.uniform(0.5, 1.5, S), (P, 1)).astype(np.float32),
        "offs": striped(np.random.permutation(T)[:S]),
        "pos1": striped(np.random.permutation(V)[:S]),
    }


def reference(xT, w1, w2, gate, offs, pos1):
    h = relu(mxq(f64(w1), 0, "e4m3").T @ mxq(f64(xT)[:, unstriped(offs)], 0, "e4m3"))
    z = np.zeros((H, V))
    z[:, unstriped(pos1)] = f64(gate)[:1] * h
    return mxq(f64(w2), 0, "e4m3").T @ mxq(z, 0, "e4m3")

@@ -1,0 +1,164 @@
+from contextlib import ExitStack
+
+import concourse.mybir as mybir
+
+K, T, S, V, H, N = 512, 1024, 512, 1024, 512, 128
+P = 128
+
+F32 = mybir.dt.float32
+BF16 = mybir.dt.bfloat16
+U32 = mybir.dt.uint32
+U16 = mybir.dt.uint16
+U8 = mybir.dt.uint8
+FP8X4 = mybir.dt.float8_e4m3fn_x4
+RELU = mybir.ActivationFunctionType.Relu
+MULT = mybir.AluOpType.mult
+
+FLOPS = 2 * H * K * S + 2 * N * H * V
+
+
+def tile_picked_voxel_relu_e_kernel(tc, xT, w1, w2, gate, offs, pos1, out):
+    nc = tc.nc
+    vcopy, scopy = nc.vector.tensor_copy, nc.scalar.copy
+    with ExitStack() as ctx:
+        held = ctx.enter_context(tc.tile_pool(name="held", bufs=1))
+        psum = ctx.enter_context(tc.psum_pool(name="psum", bufs=1))
+
+        points = held.tile([P, S // 16], U16, name="points")
+        cells = held.tile([P, S // 16], U16, name="cells")
+        gates = held.tile([P, S], F32, name="gates")
+        w2raw = held.tile([P, 4, N], F32, name="w2raw")
+        xv = xT.rearrange("(p j) w -> p j w", j=4)
+        wv = w1.rearrange("(p j) w -> p j w", j=4)
+
+        xraw = [held.tile([P, 2, T], F32, name=f"xraw{u}") for u in range(2)]
+        w1raw = held.tile([P, 4, H], F32, name="w1raw")
+        TH = T // 2
+        nc.sync.dma_start(xraw[0][:, :, 0:TH], xv[:, 0:2, 0:TH])
+        nc.sync.dma_start(points[:], offs)
+        nc.sync.dma_start(xraw[0][:, :, TH:T], xv[:, 0:2, TH:T])
+        nc.sync.dma_start(xraw[1][:, :, 0:TH], xv[:, 2:4, 0:TH])
+        nc.sync.dma_start(xraw[1][:, :, TH:T], xv[:, 2:4, TH:T])
+        for b in range(2):
+            nc.sync.dma_start(w1raw[:, 2 * b : 2 * b + 2, :], wv[:, 2 * b : 2 * b + 2, :])
+        nc.sync.dma_start(cells[:], pos1)
+        nc.sync.dma_start(gates[:], gate)
+        nc.sync.dma_start(w2raw[:], w2.rearrange("(p j) n -> p j n", j=4))
+
+        z = [held.tile([P, V], F32, name=f"z{t}") for t in range(4)]
+        warm = held.tile([P, 1], F32, name="warm")
+        warmed = held.tile([P, 1], F32, name="warmed")
+        nc.vector.memset(warm[:], 0.0)
+        nc.scalar.activation(warmed[:], warm[:], RELU)
+        nc.vector.memset(z[0][:], 0.0)
+        nc.gpsimd.memset(z[1][:], 0.0)
+        nc.vector.memset(z[2][:], 0.0)
+        nc.gpsimd.memset(z[3][:], 0.0)
+
+        pairs = [held.tile([P, T * 2], BF16, name=f"pairs{u}", align_bytes=64) for u in range(2)]
+        xg = held.tile([P, S * 4], BF16, name="xg", align_bytes=64)
+        xgw = xg[:].bitcast(U32).rearrange("p (n u) -> p n u", u=2)
+        xq = held.tile([P, S], U32, name="xq", align_bytes=64)
+        xs = held.tile([P, S], U8, name="xs", align_bytes=64)
+        w1g = held.tile([P, 4 * H], BF16, name="w1g", align_bytes=64)
+        w1q = held.tile([P, H], U32, name="w1q", align_bytes=64)
+        w1s = held.tile([P, H], U8, name="w1s", align_bytes=64)
+        w2q = held.tile([P, N], U32, name="w2q", align_bytes=64)
+        w2s = held.tile([P, N], U8, name="w2s", align_bytes=64)
+        hr = [held.tile([P, S], F32, name=f"hr{t}") for t in range(4)]
+        zg = held.tile([P, V, 4], BF16, name="zg", align_bytes=64)
+        zq = held.tile([P, V], U32, name="zq", align_bytes=64)
+        zs = held.tile([P, V], U8, name="zs", align_bytes=64)
+
+        def pair(copy, u, c0, c1):
+            copy(
+                pairs[u][:].rearrange("p (w e) -> p w e", e=2)[:, c0:c1, :],
+                xraw[u][:].rearrange("p e w -> p w e")[:, c0:c1, :],
+            )
+
+        def pick(u, n0, n1):
+            nc.vector.tensor_copy(
+                xgw[:, n0:n1, u], pairs[u][:].bitcast(U32).indirect(points[:, n0 // 16 : n1 // 16])
+            )
+
+        def quantise(codes, scales, grouped, c0, c1):
+            nc.vector.quantize_mx(
+                out=codes[:, c0:c1].bitcast(FP8X4), scales=scales[:, c0:c1], in_=grouped[:, 4 * c0 : 4 * c1]
+            )
+
+        def turn(copy, j0, j1, t0, t1):
+            copy(
+                w1g[:].rearrange("p (t m j) -> p m t j", t=4, j=4)[:, :, t0:t1, j0:j1],
+                w1raw[:].rearrange("p j (m t) -> p m t j", t=4)[:, :, t0:t1, j0:j1],
+            )
+
+        def scatter(t, n0, n1):
+            nc.vector.tensor_tensor(
+                z[t][:].indirect(cells[:, n0 // 16 : n1 // 16]), hr[t][:, n0:n1], gates[:, n0:n1], MULT
+            )
+
+        def product(acc, t, n0, n1):
+            cols = slice(128 * t, 128 * (t + 1))
+            nc.tensor.matmul_mx(
+                out=acc[:], lhsT=w1q[:, cols].bitcast(FP8X4), lhsT_scale=w1s[:, cols],
+                rhs=xq[:, n0:n1].bitcast(FP8X4), rhs_scale=xs[:, n0:n1], start=True, stop=True,
+            )
+
+        pair(vcopy, 0, 0, TH)
+        pair(vcopy, 0, TH, T)
+        pick(0, 0, S)
+        pair(scopy, 1, 0, TH)
+        pair(vcopy, 1, TH, TH + 320)
+        pair(scopy, 1, TH + 320, T)
+        SH = S // 2
+        h0 = [psum.tile([P, SH], F32, name=f"h0{a}") for a in range(2)]
+        pick(1, 0, SH)
+        turn(scopy, 0, 2, 0, 1)
+        quantise(xq, xs, xg, 0, SH)
+        pick(1, SH, S)
+        turn(scopy, 2, 4, 0, 1)
+        quantise(w1q, w1s, w1g, 0, 128)
+        turn(scopy, 0, 4, 1, 3)
+        product(h0[0], 0, 0, SH)
+        nc.scalar.activation(hr[0][:, 0:SH], h0[0][:], RELU)
+        quantise(xq, xs, xg, SH, S)
+        product(h0[1], 0, SH, S)
+        nc.scalar.activation(hr[0][:, SH:S], h0[1][:], RELU)
+        turn(vcopy, 0, 4, 3, 4)
+        scatter(0, 0, SH)
+        scatter(0, SH, S)
+        quantise(w1q, w1s, w1g, 128, 256)
+        quantise(w1q, w1s, w1g, 256, 512)
+        for t in range(1, 4):
+            ht = psum.tile([P, S], F32, name=f"h{t}")
+            product(ht, t, 0, S)
+            nc.scalar.activation(hr[t][:], ht[:], RELU)
+        w2g = held.tile([P, N * 4], BF16, name="w2g", tag="xg", align_bytes=64)
+        scopy(w2g[:].rearrange("p (n j) -> p n j", j=4), w2raw[:].rearrange("p j n -> p n j"))
+
+        for t in range(4):
+            if t > 0:
+                scatter(t, 0, S)
+            if t == 1:
+                quantise(w2q, w2s, w2g, 0, N)
+            if t < 3:
+                scopy(zg[:, :, t], z[t][:])
+
+        nc.vector.tensor_copy(zg[:, 0:512:256, 3], zg[:, 0:512:256, 2])
+        for i in range(2):
+            vcopy(zg[:, 256 * i : 256 * i + 256, 3], z[3][:, 256 * i : 256 * i + 256])
+            scopy(zg[:, 512 + 256 * i : 768 + 256 * i, 3], z[3][:, 512 + 256 * i : 768 + 256 * i])
+        zgf = zg[:].rearrange("p v t -> p (v t)")
+
+        edges = [0, 256, 512, 768, 896, 1024]
+        for i in range(5):
+            c0, c1 = edges[i], edges[i + 1]
+            quantise(zq, zs, zgf, c0, c1)
+            o = psum.tile([P, c1 - c0], F32, name=f"o{i}", tag=f"h0{i - 3}" if i > 2 else f"o{i}")
+            nc.tensor.matmul_mx(
+                out=o[:], lhsT=w2q[:].bitcast(FP8X4), lhsT_scale=w2s[:],
+                rhs=zq[:, c0:c1].bitcast(FP8X4), rhs_scale=zs[:, c0:c1], start=True, stop=True,
+            )
+            res = held.tile([P, c1 - c0], F32, name=f"res{i}")
+            (vcopy if i == 4 else scopy)(res[:], o[:])
+            nc.sync.dma_start(out[:, c0:c1], res[:])

@@ -22,139 +22,157 @@ def tile_picked_voxel_relu_e_kernel(tc, xT, w1, w2, gate, offs, pos1, out):
     vcopy, scopy = nc.vector.tensor_copy, nc.scalar.copy
     with ExitStack() as ctx:
         held = ctx.enter_context(tc.tile_pool(name="held", bufs=1))
+        reused = ctx.enter_context(tc.tile_pool(name="reused", bufs=1))
         psum = ctx.enter_context(tc.psum_pool(name="psum", bufs=1))
 
         points = held.tile([P, S // 16], U16, name="points")
         cells = held.tile([P, S // 16], U16, name="cells")
         gates = held.tile([P, S], F32, name="gates")
-        w2raw = held.tile([P, 4, N], F32, name="w2raw")
+        w2raw = held.tile([P, 4, N], F32, name="w2raw", align_bytes=64)
         xv = xT.rearrange("(p j) w -> p j w", j=4)
         wv = w1.rearrange("(p j) w -> p j w", j=4)
 
-        xraw = [held.tile([P, 2, T], F32, name=f"xraw{u}") for u in range(2)]
-        w1raw = held.tile([P, 4, H], F32, name="w1raw")
         TH = T // 2
-        nc.sync.dma_start(xraw[0][:, :, 0:TH], xv[:, 0:2, 0:TH])
+        xraw = [[held.tile([P, 2, TH], F32, name=f"xraw{u}{h}") for h in range(2)] for u in range(2)]
+        w1raw = held.tile([P, 4, H], F32, name="w1raw")
+        nc.sync.dma_start(xraw[0][0][:], xv[:, 0:2, 0:TH])
+        nc.sync.dma_start(xraw[0][1][:], xv[:, 0:2, TH:T])
         nc.sync.dma_start(points[:], offs)
-        nc.sync.dma_start(xraw[0][:, :, TH:T], xv[:, 0:2, TH:T])
-        nc.sync.dma_start(xraw[1][:, :, 0:TH], xv[:, 2:4, 0:TH])
-        nc.sync.dma_start(xraw[1][:, :, TH:T], xv[:, 2:4, TH:T])
+        nc.sync.dma_start(xraw[1][1][:], xv[:, 2:4, TH:T])
+        nc.sync.dma_start(xraw[1][0][:], xv[:, 2:4, 0:TH])
         for b in range(2):
             nc.sync.dma_start(w1raw[:, 2 * b : 2 * b + 2, :], wv[:, 2 * b : 2 * b + 2, :])
         nc.sync.dma_start(cells[:], pos1)
         nc.sync.dma_start(gates[:], gate)
-        nc.sync.dma_start(w2raw[:], w2.rearrange("(p j) n -> p j n", j=4))
+        w2v = w2.rearrange("(g t r) n -> r g t n", t=4, r=8)
+        for r in range(8):
+            nc.sync.dma_start(w2raw[r:P:8, :, :], w2v[r])
 
-        z = [held.tile([P, V], F32, name=f"z{t}") for t in range(4)]
-        warm = held.tile([P, 1], F32, name="warm")
-        warmed = held.tile([P, 1], F32, name="warmed")
-        nc.vector.memset(warm[:], 0.0)
-        nc.scalar.activation(warmed[:], warm[:], RELU)
-        nc.vector.memset(z[0][:], 0.0)
-        nc.gpsimd.memset(z[1][:], 0.0)
-        nc.vector.memset(z[2][:], 0.0)
-        nc.gpsimd.memset(z[3][:], 0.0)
+        zA = held.tile([P, V], F32, name="zA")
+        zB = held.tile([P, V], F32, name="zB")
+        nc.vector.memset(zA[:], 0.0)
+        nc.vector.memset(zB[:], 0.0)
 
-        pairs = [held.tile([P, T * 2], BF16, name=f"pairs{u}", align_bytes=64) for u in range(2)]
-        xg = held.tile([P, S * 4], BF16, name="xg", align_bytes=64)
-        xgw = xg[:].bitcast(U32).rearrange("p (n u) -> p n u", u=2)
+        SHARED = 8
+        both = reused.tile([P, 2 * (2 * T - SHARED)], BF16, name="both", align_bytes=64, offset=0)
+        pairs = [both[:, 2 * u * (T - SHARED) : 2 * u * (T - SHARED) + 2 * T] for u in range(2)]
+        SH = S // 2
+        xg = [reused.tile([P, SH * 4], BF16, name=f"xg{a}", align_bytes=64, offset=8192 + 2048 * a) for a in range(2)]
         xq = held.tile([P, S], U32, name="xq", align_bytes=64)
         xs = held.tile([P, S], U8, name="xs", align_bytes=64)
-        w1g = held.tile([P, 4 * H], BF16, name="w1g", align_bytes=64)
-        w1q = held.tile([P, H], U32, name="w1q", align_bytes=64)
-        w1s = held.tile([P, H], U8, name="w1s", align_bytes=64)
-        w2q = held.tile([P, N], U32, name="w2q", align_bytes=64)
+        w1q = [held.tile([P, 128], U32, name=f"w1q{t}", align_bytes=64) for t in range(4)]
+        w1s = [held.tile([P, 128], U8, name=f"w1s{t}", align_bytes=64) for t in range(4)]
         w2s = held.tile([P, N], U8, name="w2s", align_bytes=64)
-        hr = [held.tile([P, S], F32, name=f"hr{t}") for t in range(4)]
-        zg = held.tile([P, V, 4], BF16, name="zg", align_bytes=64)
+        hr = [held.tile([P, S], F32, name=f"hr{t}", align_bytes=64) for t in range(4)]
         zq = held.tile([P, V], U32, name="zq", align_bytes=64)
         zs = held.tile([P, V], U8, name="zs", align_bytes=64)
 
-        def pair(copy, u, c0, c1):
+        def pair(copy, u, h, c0, c1):
             copy(
-                pairs[u][:].rearrange("p (w e) -> p w e", e=2)[:, c0:c1, :],
-                xraw[u][:].rearrange("p e w -> p w e")[:, c0:c1, :],
+                pairs[u].rearrange("p (w e) -> p w e", e=2)[:, h * TH + c0 : h * TH + c1, :],
+                xraw[u][h][:].rearrange("p e w -> p w e")[:, c0:c1, :],
             )
 
-        def pick(u, n0, n1):
+        def pick(u, a):
             nc.vector.tensor_copy(
-                xgw[:, n0:n1, u], pairs[u][:].bitcast(U32).indirect(points[:, n0 // 16 : n1 // 16])
+                xg[a][:].bitcast(U32).rearrange("p (n u) -> p n u", u=2)[:, :, u],
+                pairs[u].bitcast(U32).indirect(points[:, a * SH // 16 : (a + 1) * SH // 16]),
             )
+
+        def quantise_x(a):
+            quantise(xq[:, a * SH : (a + 1) * SH], xs[:, a * SH : (a + 1) * SH], xg[a], 0, SH)
 
         def quantise(codes, scales, grouped, c0, c1):
             nc.vector.quantize_mx(
                 out=codes[:, c0:c1].bitcast(FP8X4), scales=scales[:, c0:c1], in_=grouped[:, 4 * c0 : 4 * c1]
             )
 
-        def turn(copy, j0, j1, t0, t1):
+        def quantise_w1(t):
+            quantise(w1q[t], w1s[t], w1g[t], 0, 128)
+
+        def turn(copy, t):
             copy(
-                w1g[:].rearrange("p (t m j) -> p m t j", t=4, j=4)[:, :, t0:t1, j0:j1],
-                w1raw[:].rearrange("p j (m t) -> p m t j", t=4)[:, :, t0:t1, j0:j1],
+                w1g[t][:].rearrange("p (g r j) -> p g r j", r=8, j=4),
+                w1raw[:].rearrange("p j (g t r) -> p t g r j", t=4, r=8)[:, t],
             )
 
-        def scatter(t, n0, n1):
+        def scatter(window, t, n0, n1):
             nc.vector.tensor_tensor(
-                z[t][:].indirect(cells[:, n0 // 16 : n1 // 16]), hr[t][:, n0:n1], gates[:, n0:n1], MULT
+                window[:].indirect(cells[:, n0 // 16 : n1 // 16]), hr[t][:, n0:n1], gates[:, n0:n1], MULT
             )
 
-        def product(acc, t, n0, n1):
-            cols = slice(128 * t, 128 * (t + 1))
-            nc.tensor.matmul_mx(
-                out=acc[:], lhsT=w1q[:, cols].bitcast(FP8X4), lhsT_scale=w1s[:, cols],
-                rhs=xq[:, n0:n1].bitcast(FP8X4), rhs_scale=xs[:, n0:n1], start=True, stop=True,
-            )
+        def layer1(name, t, edges):
+            acc = psum.tile([P, edges[-1] - edges[0]], F32, name=name, tag="even" if t in (A, C) else "odd")
+            for n0, n1 in zip(edges, edges[1:]):
+                nc.tensor.matmul_mx(
+                    out=acc[:, n0 - edges[0] : n1 - edges[0]], lhsT=w1q[t][:].bitcast(FP8X4),
+                    lhsT_scale=w1s[t][:], rhs=xq[:, n0:n1].bitcast(FP8X4), rhs_scale=xs[:, n0:n1],
+                    start=True, stop=True,
+                )
+            nc.scalar.activation(hr[t][:, edges[0] : edges[-1]], acc[:], RELU)
 
-        pair(vcopy, 0, 0, TH)
-        pair(vcopy, 0, TH, T)
-        pick(0, 0, S)
-        pair(scopy, 1, 0, TH)
-        pair(vcopy, 1, TH, TH + 320)
-        pair(scopy, 1, TH + 320, T)
-        SH = S // 2
-        h0 = [psum.tile([P, SH], F32, name=f"h0{a}") for a in range(2)]
-        pick(1, 0, SH)
-        turn(scopy, 0, 2, 0, 1)
-        quantise(xq, xs, xg, 0, SH)
-        pick(1, SH, S)
-        turn(scopy, 2, 4, 0, 1)
-        quantise(w1q, w1s, w1g, 0, 128)
-        turn(scopy, 0, 4, 1, 3)
-        product(h0[0], 0, 0, SH)
-        nc.scalar.activation(hr[0][:, 0:SH], h0[0][:], RELU)
-        quantise(xq, xs, xg, SH, S)
-        product(h0[1], 0, SH, S)
-        nc.scalar.activation(hr[0][:, SH:S], h0[1][:], RELU)
-        turn(vcopy, 0, 4, 3, 4)
-        scatter(0, 0, SH)
-        scatter(0, SH, S)
-        quantise(w1q, w1s, w1g, 128, 256)
-        quantise(w1q, w1s, w1g, 256, 512)
-        for t in range(1, 4):
-            ht = psum.tile([P, S], F32, name=f"h{t}")
-            product(ht, t, 0, S)
-            nc.scalar.activation(hr[t][:], ht[:], RELU)
-        w2g = held.tile([P, N * 4], BF16, name="w2g", tag="xg", align_bytes=64)
+        A, B, C, D = 3, 0, 1, 2
+        for h in range(2):
+            pair(vcopy, 0, h, 0, 352)
+            pair(scopy, 0, h, 352, TH)
+        pick(0, 0)
+        pick(0, 1)
+        pair(scopy, 1, 1, 0, TH)
+        pair(vcopy, 1, 0, 0, 352)
+        pair(scopy, 1, 0, 352, TH)
+        pick(1, 0)
+        pick(1, 1)
+        quantise_x(0)
+        quantise_x(1)
+        places = {A: 0, B: 8192, D: 9216, C: 10240}
+        w1g = {t: reused.tile([P, H], BF16, name=f"w1g{t}", align_bytes=64, offset=places[t]) for t in places}
+        turn(scopy, A)
+        turn(scopy, B)
+        turn(scopy, C)
+        turn(vcopy, D)
+        quantise_w1(A)
+        layer1("hA0", A, [0, 128])
+        quantise_w1(D)
+        quantise_w1(B)
+        layer1("hB0", B, [0, 128])
+        quantise_w1(C)
+        layer1("hA1", A, [128, 256, S])
+        layer1("hB1", B, [128, 256, S])
+        layer1("hC", C, [0, S])
+        layer1("hD", D, [0, S])
+
+        zC = reused.tile([P, V], F32, name="zC", align_bytes=64, offset=places[C])
+        nc.gpsimd.memset(zC[:], 0.0)
+        zD = held.tile([P, 2 * V], F32, name="zD", tag=f"w1q{B}", align_bytes=64)
+        nc.gpsimd.memset(zD[:, 0:V], 0.0)
+        scatter(zA, A, 0, 128)
+        scatter(zB, B, 0, 128)
+        scatter(zA, A, 128, S)
+        nc.sync.dma_start(zD[:, V : 2 * V], zA[:])
+        w2g = held.tile([P, N * 4], BF16, name="w2g", tag=f"w1q{C}", align_bytes=64)
         scopy(w2g[:].rearrange("p (n j) -> p n j", j=4), w2raw[:].rearrange("p j n -> p n j"))
-
-        for t in range(4):
-            if t > 0:
-                scatter(t, 0, S)
-            if t == 1:
-                quantise(w2q, w2s, w2g, 0, N)
-            if t < 3:
-                scopy(zg[:, :, t], z[t][:])
-
-        nc.vector.tensor_copy(zg[:, 0:512:256, 3], zg[:, 0:512:256, 2])
+        scatter(zB, B, 128, S)
+        zg = held.tile([P, V, 4], BF16, name="zg", tag="w2raw", align_bytes=64)
+        w2q = held.tile([P, N], U32, name="w2q", tag=f"hr{B}", align_bytes=64)
+        scopy(zg[:, :, B], zB[:])
+        scatter(zC, C, 0, S)
         for i in range(2):
-            vcopy(zg[:, 256 * i : 256 * i + 256, 3], z[3][:, 256 * i : 256 * i + 256])
-            scopy(zg[:, 512 + 256 * i : 768 + 256 * i, 3], z[3][:, 512 + 256 * i : 768 + 256 * i])
+            scopy(zg[:, 512 * i : 512 * i + 512, C], zC[:, 512 * i : 512 * i + 512])
+        scatter(zD, D, 0, S)
+        quantise(w2q, w2s, w2g, 0, N)
+
+        zDv = zD[:].rearrange("p (e c) -> p c e", e=2)
+        for i in range(2):
+            vcopy(zg[:, 256 * i : 256 * i + 256, 2:4], zDv[:, 256 * i : 256 * i + 256, :])
+            scopy(zg[:, 512 + 256 * i : 768 + 256 * i, 2:4], zDv[:, 512 + 256 * i : 768 + 256 * i, :])
         zgf = zg[:].rearrange("p v t -> p (v t)")
 
         edges = [0, 256, 512, 768, 896, 1024]
+        banks = ["o0", "o1", "o2", "o3", "o4"]
         for i in range(5):
             c0, c1 = edges[i], edges[i + 1]
             quantise(zq, zs, zgf, c0, c1)
-            o = psum.tile([P, c1 - c0], F32, name=f"o{i}", tag=f"h0{i - 3}" if i > 2 else f"o{i}")
+            o = psum.tile([P, c1 - c0], F32, name=f"o{i}", tag=banks[i])
             nc.tensor.matmul_mx(
                 out=o[:], lhsT=w2q[:].bitcast(FP8X4), lhsT_scale=w2s[:],
                 rhs=zq[:, c0:c1].bitcast(FP8X4), rhs_scale=zs[:, c0:c1], start=True, stop=True,

@@ -50,8 +50,12 @@ def tile_picked_voxel_relu_e_kernel(tc, xT, w1, w2, gate, offs, pos1, out):
 
         zA = held.tile([P, V], F32, name="zA")
         zB = held.tile([P, V], F32, name="zB")
+        zC = held.tile([P, V], F32, name="zC")
+        zD = held.tile([P, 2 * V], F32, name="zD")
         nc.vector.memset(zA[:], 0.0)
+        nc.gpsimd.memset(zC[:], 0.0)
         nc.vector.memset(zB[:], 0.0)
+        nc.gpsimd.memset(zD[:, 0:V], 0.0)
 
         SHARED = 8
         both = reused.tile([P, 2 * (2 * T - SHARED)], BF16, name="both", align_bytes=64, offset=0)
@@ -141,10 +145,6 @@ def tile_picked_voxel_relu_e_kernel(tc, xT, w1, w2, gate, offs, pos1, out):
         layer1("hC", C, [0, S])
         layer1("hD", D, [0, S])
 
-        zC = reused.tile([P, V], F32, name="zC", align_bytes=64, offset=places[C])
-        nc.gpsimd.memset(zC[:], 0.0)
-        zD = held.tile([P, 2 * V], F32, name="zD", tag=f"w1q{B}", align_bytes=64)
-        nc.gpsimd.memset(zD[:, 0:V], 0.0)
         scatter(zA, A, 0, 128)
         scatter(zB, B, 0, 128)
         scatter(zA, A, 128, S)

@@ -33,7 +33,10 @@ def tile_picked_voxel_relu_e_kernel(tc, xT, w1, w2, gate, offs, pos1, out):
         wv = w1.rearrange("(p j) w -> p j w", j=4)
 
         TH = T // 2
-        xraw = [[held.tile([P, 2, TH], F32, name=f"xraw{u}{h}") for h in range(2)] for u in range(2)]
+        xraw = [
+            [held.tile([P, 2, TH], F32, name=f"xraw0{h}") for h in range(2)],
+            [reused.tile([P, 2, TH], F32, name="xraw10", align_bytes=64, offset=12288), held.tile([P, 2, TH], F32, name="xraw11")],
+        ]
         w1raw = held.tile([P, 4, H], F32, name="w1raw")
         nc.sync.dma_start(xraw[0][0][:], xv[:, 0:2, 0:TH])
         nc.sync.dma_start(xraw[0][1][:], xv[:, 0:2, TH:T])
@@ -51,7 +54,7 @@ def tile_picked_voxel_relu_e_kernel(tc, xT, w1, w2, gate, offs, pos1, out):
         zA = held.tile([P, V], F32, name="zA")
         zB = held.tile([P, V], F32, name="zB")
         zC = held.tile([P, V], F32, name="zC")
-        zD = held.tile([P, 2 * V], F32, name="zD")
+        zD = held.tile([P, V + 512], F32, name="zD")
         nc.vector.memset(zA[:], 0.0)
         nc.gpsimd.memset(zC[:], 0.0)
         nc.vector.memset(zB[:], 0.0)
@@ -64,7 +67,7 @@ def tile_picked_voxel_relu_e_kernel(tc, xT, w1, w2, gate, offs, pos1, out):
         xg = [reused.tile([P, SH * 4], BF16, name=f"xg{a}", align_bytes=64, offset=8192 + 2048 * a) for a in range(2)]
         xq = held.tile([P, S], U32, name="xq", align_bytes=64)
         xs = held.tile([P, S], U8, name="xs", align_bytes=64)
-        w1q = [held.tile([P, 128], U32, name=f"w1q{t}", align_bytes=64) for t in range(4)]
+        w1q = {t: held.tile([P, 128], U32, name=f"w1q{t}", align_bytes=64) for t in range(3)}
         w1s = [held.tile([P, 128], U8, name=f"w1s{t}", align_bytes=64) for t in range(4)]
         w2s = held.tile([P, N], U8, name="w2s", align_bytes=64)
         hr = [held.tile([P, S], F32, name=f"hr{t}", align_bytes=64) for t in range(4)]
@@ -96,8 +99,8 @@ def tile_picked_voxel_relu_e_kernel(tc, xT, w1, w2, gate, offs, pos1, out):
 
         def turn(copy, t):
             copy(
-                w1g[t][:].rearrange("p (g r j) -> p g r j", r=8, j=4),
-                w1raw[:].rearrange("p j (g t r) -> p t g r j", t=4, r=8)[:, t],
+                w1g[t][:].rearrange("p (g r i j) -> p g r j i", r=2, i=4, j=4),
+                w1raw[:].rearrange("p j (g t r i) -> p t g r j i", t=4, r=2, i=4)[:, t],
             )
 
         def scatter(window, t, n0, n1):
@@ -128,16 +131,17 @@ def tile_picked_voxel_relu_e_kernel(tc, xT, w1, w2, gate, offs, pos1, out):
         pick(1, 1)
         quantise_x(0)
         quantise_x(1)
-        places = {A: 0, B: 8192, D: 9216, C: 10240}
+        places = {A: 12288, B: 0, C: 8192, D: 10240}
         w1g = {t: reused.tile([P, H], BF16, name=f"w1g{t}", align_bytes=64, offset=places[t]) for t in places}
         turn(scopy, A)
         turn(scopy, B)
         turn(scopy, C)
-        turn(vcopy, D)
+        w1q[A] = reused.tile([P, 128], U32, name="w1q3", align_bytes=64, offset=9216)
         quantise_w1(A)
+        turn(vcopy, D)
         layer1("hA0", A, [0, 128])
-        quantise_w1(D)
         quantise_w1(B)
+        quantise_w1(D)
         layer1("hB0", B, [0, 128])
         quantise_w1(C)
         layer1("hA1", A, [128, 256, S])
@@ -148,11 +152,12 @@ def tile_picked_voxel_relu_e_kernel(tc, xT, w1, w2, gate, offs, pos1, out):
         scatter(zA, A, 0, 128)
         scatter(zB, B, 0, 128)
         scatter(zA, A, 128, S)
-        nc.sync.dma_start(zD[:, V : 2 * V], zA[:])
+        nc.sync.dma_start(zD[:, V : V + 512], zA[:, 0:512])
         w2g = held.tile([P, N * 4], BF16, name="w2g", tag=f"w1q{C}", align_bytes=64)
         scopy(w2g[:].rearrange("p (n j) -> p n j", j=4), w2raw[:].rearrange("p j n -> p n j"))
-        scatter(zB, B, 128, S)
         zg = held.tile([P, V, 4], BF16, name="zg", tag="w2raw", align_bytes=64)
+        scopy(zg[:, 512:V, A], zA[:, 512:V])
+        scatter(zB, B, 128, S)
         w2q = held.tile([P, N], U32, name="w2q", tag=f"hr{B}", align_bytes=64)
         scopy(zg[:, :, B], zB[:])
         scatter(zC, C, 0, S)
@@ -161,10 +166,10 @@ def tile_picked_voxel_relu_e_kernel(tc, xT, w1, w2, gate, offs, pos1, out):
         scatter(zD, D, 0, S)
         quantise(w2q, w2s, w2g, 0, N)
 
-        zDv = zD[:].rearrange("p (e c) -> p c e", e=2)
+        zDv = zD[:].rearrange("p (e c) -> p c e", c=512)[:, :, 0:3:2]
         for i in range(2):
             vcopy(zg[:, 256 * i : 256 * i + 256, 2:4], zDv[:, 256 * i : 256 * i + 256, :])
-            scopy(zg[:, 512 + 256 * i : 768 + 256 * i, 2:4], zDv[:, 512 + 256 * i : 768 + 256 * i, :])
+            scopy(zg[:, 512 + 256 * i : 768 + 256 * i, D], zD[:, 512 + 256 * i : 768 + 256 * i])
         zgf = zg[:].rearrange("p v t -> p (v t)")
 
         edges = [0, 256, 512, 768, 896, 1024]

@@ -55,6 +55,10 @@ def tile_picked_voxel_relu_e_kernel(tc, xT, w1, w2, gate, offs, pos1, out):
         zB = held.tile([P, V], F32, name="zB")
         zC = held.tile([P, V], F32, name="zC")
         zD = held.tile([P, V + 512], F32, name="zD")
+        warm = held.tile([P, 1], F32, name="warm")
+        warmed = held.tile([P, 1], F32, name="warmed")
+        nc.vector.memset(warm[:], 0.0)
+        nc.scalar.activation(warmed[:], warm[:], RELU)
         nc.vector.memset(zA[:], 0.0)
         nc.gpsimd.memset(zC[:], 0.0)
         nc.vector.memset(zB[:], 0.0)

@@ -34,7 +34,7 @@ def tile_picked_voxel_relu_e_kernel(tc, xT, w1, w2, gate, offs, pos1, out):
 
         TH = T // 2
         xraw = [
-            [held.tile([P, 2, TH], F32, name=f"xraw0{h}") for h in range(2)],
+            [reused.tile([P, 2, TH], F32, name="xraw00", align_bytes=64, offset=0), held.tile([P, 2, TH], F32, name="xraw01")],
             [reused.tile([P, 2, TH], F32, name="xraw10", align_bytes=64, offset=12288), held.tile([P, 2, TH], F32, name="xraw11")],
         ]
         w1raw = held.tile([P, 4, H], F32, name="w1raw")
@@ -64,9 +64,7 @@ def tile_picked_voxel_relu_e_kernel(tc, xT, w1, w2, gate, offs, pos1, out):
         nc.vector.memset(zB[:], 0.0)
         nc.gpsimd.memset(zD[:, 0:V], 0.0)
 
-        SHARED = 8
-        both = reused.tile([P, 2 * (2 * T - SHARED)], BF16, name="both", align_bytes=64, offset=0)
-        pairs = [both[:, 2 * u * (T - SHARED) : 2 * u * (T - SHARED) + 2 * T] for u in range(2)]
+        pairs = [held.tile([P, 2 * T], BF16, name="pairs0", align_bytes=64)[:]]
         SH = S // 2
         xg = [reused.tile([P, SH * 4], BF16, name=f"xg{a}", align_bytes=64, offset=8192 + 2048 * a) for a in range(2)]
         xq = held.tile([P, S], U32, name="xq", align_bytes=64)
@@ -103,7 +101,7 @@ def tile_picked_voxel_relu_e_kernel(tc, xT, w1, w2, gate, offs, pos1, out):
 
         def turn(copy, t):
             copy(
-                w1g[t][:].rearrange("p (g r i j) -> p g r j i", r=2, i=4, j=4),
+                w1g[t].rearrange("p (g r i j) -> p g r j i", r=2, i=4, j=4),
                 w1raw[:].rearrange("p j (g t r i) -> p t g r j i", t=4, r=2, i=4)[:, t],
             )
 
@@ -128,6 +126,7 @@ def tile_picked_voxel_relu_e_kernel(tc, xT, w1, w2, gate, offs, pos1, out):
             pair(scopy, 0, h, 352, TH)
         pick(0, 0)
         pick(0, 1)
+        pairs.append(reused.tile([P, 2 * T], BF16, name="pairs1", align_bytes=64, offset=0)[:])
         pair(scopy, 1, 1, 0, TH)
         pair(vcopy, 1, 0, 0, 352)
         pair(scopy, 1, 0, 352, TH)
@@ -135,8 +134,10 @@ def tile_picked_voxel_relu_e_kernel(tc, xT, w1, w2, gate, offs, pos1, out):
         pick(1, 1)
         quantise_x(0)
         quantise_x(1)
-        places = {A: 12288, B: 0, C: 8192, D: 10240}
-        w1g = {t: reused.tile([P, H], BF16, name=f"w1g{t}", align_bytes=64, offset=places[t]) for t in places}
+        places = {B: 0, C: 8192}
+        w1g = {t: reused.tile([P, H], BF16, name=f"w1g{t}", align_bytes=64, offset=places[t])[:] for t in places}
+        outer = reused.tile([P, 2 * H], BF16, name="outer", align_bytes=64, offset=12288)
+        w1g[A], w1g[D] = outer[:, 0:H], outer[:, H : 2 * H]
         turn(scopy, A)
         turn(scopy, B)
         turn(scopy, C)

@@ -99,10 +99,10 @@ def tile_picked_voxel_relu_e_kernel(tc, xT, w1, w2, gate, offs, pos1, out):
         def quantise_w1(t):
             quantise(w1q[t], w1s[t], w1g[t], 0, 128)
 
-        def turn(copy, t):
+        def turn(copy, t, j0=0, j1=4):
             copy(
-                w1g[t].rearrange("p (g r i j) -> p g r j i", r=2, i=4, j=4),
-                w1raw[:].rearrange("p j (g t r i) -> p t g r j i", t=4, r=2, i=4)[:, t],
+                w1g[t].rearrange("p (g r i j) -> p g r j i", r=2, i=4, j=4)[:, :, :, j0:j1],
+                w1raw[:].rearrange("p j (g t r i) -> p t g r j i", t=4, r=2, i=4)[:, t, :, :, j0:j1],
             )
 
         def scatter(window, t, n0, n1):
@@ -134,21 +134,21 @@ def tile_picked_voxel_relu_e_kernel(tc, xT, w1, w2, gate, offs, pos1, out):
         pick(1, 1)
         quantise_x(0)
         quantise_x(1)
-        places = {B: 0, C: 8192}
-        w1g = {t: reused.tile([P, H], BF16, name=f"w1g{t}", align_bytes=64, offset=places[t])[:] for t in places}
-        outer = reused.tile([P, 2 * H], BF16, name="outer", align_bytes=64, offset=12288)
-        w1g[A], w1g[D] = outer[:, 0:H], outer[:, H : 2 * H]
-        turn(scopy, A)
+        w1g = {t: reused.tile([P, H], BF16, name=f"w1g{t}", align_bytes=64, offset=at)[:] for t, at in ((A, 12288), (C, 13312), (B, 14336))}
+        turn(scopy, A, 0, 2)
+        turn(scopy, C, 0, 2)
+        turn(scopy, A, 2, 4)
         turn(scopy, B)
-        turn(scopy, C)
-        w1q[A] = reused.tile([P, 128], U32, name="w1q3", align_bytes=64, offset=9216)
+        turn(scopy, C, 2, 4)
+        w1q[A] = reused.tile([P, 128], U32, name="w1q3", align_bytes=64, offset=0)
         quantise_w1(A)
-        turn(vcopy, D)
         layer1("hA0", A, [0, 128])
         quantise_w1(B)
-        quantise_w1(D)
+        w1g[D] = reused.tile([P, H], BF16, name="w1g2", align_bytes=64, offset=12288)[:]
+        turn(vcopy, D)
         layer1("hB0", B, [0, 128])
         quantise_w1(C)
+        quantise_w1(D)
         layer1("hA1", A, [128, 256, S])
         layer1("hB1", B, [128, 256, S])
         layer1("hC", C, [0, S])

@@ -32,14 +32,13 @@ def tile_picked_voxel_relu_e_kernel(tc, xT, w1, w2, gate, offs, pos1, out):
         xv = xT.rearrange("(p j) w -> p j w", j=4)
         wv = w1.rearrange("(p j) w -> p j w", j=4)
 
-        TH = T // 2
+        TH = 576
         xraw = [
-            [reused.tile([P, 2, TH], F32, name="xraw00", align_bytes=64, offset=0), held.tile([P, 2, TH], F32, name="xraw01")],
-            [reused.tile([P, 2, TH], F32, name="xraw10", align_bytes=64, offset=12288), held.tile([P, 2, TH], F32, name="xraw11")],
+            [held.tile([P, 2, T], F32, name="xraw0", align_bytes=64)],
+            [reused.tile([P, 2, TH], F32, name="xraw10", align_bytes=64, offset=12288), held.tile([P, 2, T - TH], F32, name="xraw11")],
         ]
         w1raw = held.tile([P, 4, H], F32, name="w1raw")
-        nc.sync.dma_start(xraw[0][0][:], xv[:, 0:2, 0:TH])
-        nc.sync.dma_start(xraw[0][1][:], xv[:, 0:2, TH:T])
+        nc.sync.dma_start(xraw[0][0][:], xv[:, 0:2, :])
         nc.sync.dma_start(points[:], offs)
         nc.sync.dma_start(xraw[1][1][:], xv[:, 2:4, TH:T])
         nc.sync.dma_start(xraw[1][0][:], xv[:, 2:4, 0:TH])
@@ -121,15 +120,14 @@ def tile_picked_voxel_relu_e_kernel(tc, xT, w1, w2, gate, offs, pos1, out):
             nc.scalar.activation(hr[t][:, edges[0] : edges[-1]], acc[:], RELU)
 
         A, B, C, D = 3, 0, 1, 2
-        for h in range(2):
-            pair(vcopy, 0, h, 0, 352)
-            pair(scopy, 0, h, 352, TH)
+        pair(vcopy, 0, 0, 0, 704)
+        pair(scopy, 0, 0, 704, T)
         pick(0, 0)
         pick(0, 1)
-        pairs.append(reused.tile([P, 2 * T], BF16, name="pairs1", align_bytes=64, offset=0)[:])
-        pair(scopy, 1, 1, 0, TH)
-        pair(vcopy, 1, 0, 0, 352)
-        pair(scopy, 1, 0, 352, TH)
+        pairs.append(held.tile([P, 2 * T], BF16, name="pairs1", tag="xraw0", align_bytes=64)[:])
+        pair(scopy, 1, 1, 0, T - TH)
+        pair(vcopy, 1, 0, 0, 384)
+        pair(scopy, 1, 0, 384, TH)
         pick(1, 0)
         pick(1, 1)
         quantise_x(0)
@@ -140,7 +138,7 @@ def tile_picked_voxel_relu_e_kernel(tc, xT, w1, w2, gate, offs, pos1, out):
         turn(scopy, A, 2, 4)
         turn(scopy, B)
         turn(scopy, C, 2, 4)
-        w1q[A] = reused.tile([P, 128], U32, name="w1q3", align_bytes=64, offset=0)
+        w1q[A] = held.tile([P, 128], U32, name="w1q3", tag="xraw0", align_bytes=64)
         quantise_w1(A)
         layer1("hA0", A, [0, 128])
         quantise_w1(B)

@@ -11,8 +11,10 @@ U32 = mybir.dt.uint32
 U16 = mybir.dt.uint16
 U8 = mybir.dt.uint8
 FP8X4 = mybir.dt.float8_e4m3fn_x4
-RELU = mybir.ActivationFunctionType.Relu
+COPY = mybir.ActivationFunctionType.Copy
 MULT = mybir.AluOpType.mult
+MAX = mybir.AluOpType.max
+ADD = mybir.AluOpType.add
 
 FLOPS = 2 * H * K * S + 2 * N * H * V
 
@@ -20,6 +22,10 @@ FLOPS = 2 * H * K * S + 2 * N * H * V
 def tile_picked_voxel_relu_e_kernel(tc, xT, w1, w2, gate, offs, pos1, out):
     nc = tc.nc
     vcopy, scopy = nc.vector.tensor_copy, nc.scalar.copy
+
+    def acopy(dst, src):
+        nc.scalar.activation(dst, src, COPY)
+
     with ExitStack() as ctx:
         held = ctx.enter_context(tc.tile_pool(name="held", bufs=1))
         reused = ctx.enter_context(tc.tile_pool(name="reused", bufs=1))
@@ -28,7 +34,7 @@ def tile_picked_voxel_relu_e_kernel(tc, xT, w1, w2, gate, offs, pos1, out):
         points = held.tile([P, S // 16], U16, name="points")
         cells = held.tile([P, S // 16], U16, name="cells")
         gates = held.tile([P, S], F32, name="gates")
-        w2raw = held.tile([P, 4, N], F32, name="w2raw", align_bytes=64)
+        w2raw = reused.tile([P, 4, N], F32, name="w2raw", align_bytes=64, offset=20480 + 3072)
         xv = xT.rearrange("(p j) w -> p j w", j=4)
         wv = w1.rearrange("(p j) w -> p j w", j=4)
 
@@ -44,34 +50,28 @@ def tile_picked_voxel_relu_e_kernel(tc, xT, w1, w2, gate, offs, pos1, out):
         nc.sync.dma_start(xraw[1][0][:], xv[:, 2:4, 0:TH])
         for b in range(2):
             nc.sync.dma_start(w1raw[:, 2 * b : 2 * b + 2, :], wv[:, 2 * b : 2 * b + 2, :])
-        nc.sync.dma_start(cells[:], pos1)
         nc.sync.dma_start(gates[:], gate)
+        nc.sync.dma_start(cells[:], pos1)
         w2v = w2.rearrange("(g t r) n -> r g t n", t=4, r=8)
         for r in range(8):
             nc.sync.dma_start(w2raw[r:P:8, :, :], w2v[r])
 
-        zA = held.tile([P, V], F32, name="zA")
-        zB = held.tile([P, V], F32, name="zB")
-        zC = held.tile([P, V], F32, name="zC")
-        zD = held.tile([P, V + 512], F32, name="zD")
-        warm = held.tile([P, 1], F32, name="warm")
-        warmed = held.tile([P, 1], F32, name="warmed")
-        nc.vector.memset(warm[:], 0.0)
-        nc.scalar.activation(warmed[:], warm[:], RELU)
-        nc.vector.memset(zA[:], 0.0)
-        nc.gpsimd.memset(zC[:], 0.0)
-        nc.vector.memset(zB[:], 0.0)
-        nc.gpsimd.memset(zD[:, 0:V], 0.0)
+        A, D, C, B = 0, 1, 2, 3
+        z = [held.tile([P, V], F32, name=f"z{t}") for t in range(4)]
+        nc.vector.memset(z[A][:], 0.0)
+        nc.gpsimd.memset(z[C][:], 0.0)
+        nc.vector.memset(z[B][:], 0.0)
+        nc.gpsimd.memset(z[D][:], 0.0)
 
         pairs = [held.tile([P, 2 * T], BF16, name="pairs0", align_bytes=64)[:]]
         SH = S // 2
         xg = [reused.tile([P, SH * 4], BF16, name=f"xg{a}", align_bytes=64, offset=8192 + 2048 * a) for a in range(2)]
         xq = held.tile([P, S], U32, name="xq", align_bytes=64)
         xs = held.tile([P, S], U8, name="xs", align_bytes=64)
-        w1q = {t: held.tile([P, 128], U32, name=f"w1q{t}", align_bytes=64) for t in range(3)}
+        w1q = {t: held.tile([P, 128], U32, name=f"w1q{t}", align_bytes=64) for t in (B, C, D)}
         w1s = [held.tile([P, 128], U8, name=f"w1s{t}", align_bytes=64) for t in range(4)]
         w2s = held.tile([P, N], U8, name="w2s", align_bytes=64)
-        hr = [held.tile([P, S], F32, name=f"hr{t}", align_bytes=64) for t in range(4)]
+        hg = [held.tile([P, S], F32, name=f"hg{t}", align_bytes=64) for t in range(4)]
         zq = held.tile([P, V], U32, name="zq", align_bytes=64)
         zs = held.tile([P, V], U8, name="zs", align_bytes=64)
 
@@ -92,11 +92,11 @@ def tile_picked_voxel_relu_e_kernel(tc, xT, w1, w2, gate, offs, pos1, out):
 
         def quantise(codes, scales, grouped, c0, c1):
             nc.vector.quantize_mx(
-                out=codes[:, c0:c1].bitcast(FP8X4), scales=scales[:, c0:c1], in_=grouped[:, 4 * c0 : 4 * c1]
+                out=codes.bitcast(FP8X4), scales=scales, in_=grouped[:, 4 * c0 : 4 * c1]
             )
 
         def quantise_w1(t):
-            quantise(w1q[t], w1s[t], w1g[t], 0, 128)
+            quantise(w1q[t][:], w1s[t][:], w1g[t], 0, 128)
 
         def turn(copy, t, j0=0, j1=4):
             copy(
@@ -104,24 +104,23 @@ def tile_picked_voxel_relu_e_kernel(tc, xT, w1, w2, gate, offs, pos1, out):
                 w1raw[:].rearrange("p j (g t r i) -> p t g r j i", t=4, r=2, i=4)[:, t, :, :, j0:j1],
             )
 
-        def scatter(window, t, n0, n1):
-            nc.vector.tensor_tensor(
-                window[:].indirect(cells[:, n0 // 16 : n1 // 16]), hr[t][:, n0:n1], gates[:, n0:n1], MULT
-            )
+        def scatter(copy, t, n0, n1):
+            copy(z[t][:].indirect(cells[:, n0 // 16 : n1 // 16]), hg[t][:, n0:n1])
 
         def layer1(name, t, edges):
-            acc = psum.tile([P, edges[-1] - edges[0]], F32, name=name, tag="even" if t in (A, C) else "odd")
+            acc = psum.tile([P, edges[-1] - edges[0]], F32, name=name)
             for n0, n1 in zip(edges, edges[1:]):
                 nc.tensor.matmul_mx(
                     out=acc[:, n0 - edges[0] : n1 - edges[0]], lhsT=w1q[t][:].bitcast(FP8X4),
                     lhsT_scale=w1s[t][:], rhs=xq[:, n0:n1].bitcast(FP8X4), rhs_scale=xs[:, n0:n1],
                     start=True, stop=True,
                 )
-            nc.scalar.activation(hr[t][:, edges[0] : edges[-1]], acc[:], RELU)
+            nc.vector.scalar_tensor_tensor(
+                hg[t][:, edges[0] : edges[-1]], acc[:], 0.0, gates[:, edges[0] : edges[-1]], MAX, MULT
+            )
 
-        A, B, C, D = 3, 0, 1, 2
         pair(vcopy, 0, 0, 0, 704)
-        pair(scopy, 0, 0, 704, T)
+        pair(acopy, 0, 0, 704, T)
         pick(0, 0)
         pick(0, 1)
         pairs.append(held.tile([P, 2 * T], BF16, name="pairs1", tag="xraw0", align_bytes=64)[:])
@@ -138,53 +137,72 @@ def tile_picked_voxel_relu_e_kernel(tc, xT, w1, w2, gate, offs, pos1, out):
         turn(scopy, A, 2, 4)
         turn(scopy, B)
         turn(scopy, C, 2, 4)
-        w1q[A] = held.tile([P, 128], U32, name="w1q3", tag="xraw0", align_bytes=64)
+        w1q[A] = held.tile([P, 128], U32, name="w1qA", tag="xraw0", align_bytes=64)
         quantise_w1(A)
-        layer1("hA0", A, [0, 128])
+        layer1("h0", A, [0, 128])
         quantise_w1(B)
-        w1g[D] = reused.tile([P, H], BF16, name="w1g2", align_bytes=64, offset=12288)[:]
+        w1g[D] = reused.tile([P, H], BF16, name="w1gD", align_bytes=64, offset=12288)[:]
         turn(vcopy, D)
-        layer1("hB0", B, [0, 128])
+        layer1("h1", B, [0, 128])
+        scatter(acopy, A, 0, 128)
+        scatter(acopy, B, 0, 128)
         quantise_w1(C)
         quantise_w1(D)
-        layer1("hA1", A, [128, 256, S])
-        layer1("hB1", B, [128, 256, S])
-        layer1("hC", C, [0, S])
-        layer1("hD", D, [0, S])
+        layer1("h2", A, [128, 256, S])
+        scatter(acopy, A, 128, S)
+        layer1("h3", C, [0, S])
+        scatter(acopy, C, 0, 320)
+        layer1("h4", D, [0, S])
+        scatter(vcopy, D, 0, S)
+        layer1("h5", B, [128, 256, S])
+        scatter(acopy, B, 128, S)
+        scatter(vcopy, C, 320, S)
 
-        scatter(zA, A, 0, 128)
-        scatter(zB, B, 0, 128)
-        scatter(zA, A, 128, S)
-        nc.sync.dma_start(zD[:, V : V + 512], zA[:, 0:512])
-        w2g = held.tile([P, N * 4], BF16, name="w2g", tag=f"w1q{C}", align_bytes=64)
-        scopy(w2g[:].rearrange("p (n j) -> p n j", j=4), w2raw[:].rearrange("p j n -> p n j"))
-        zg = held.tile([P, V, 4], BF16, name="zg", tag="w2raw", align_bytes=64)
-        scopy(zg[:, 512:V, A], zA[:, 512:V])
-        scatter(zB, B, 128, S)
-        w2q = held.tile([P, N], U32, name="w2q", tag=f"hr{B}", align_bytes=64)
-        scopy(zg[:, :, B], zB[:])
-        scatter(zC, C, 0, S)
-        for i in range(2):
-            scopy(zg[:, 512 * i : 512 * i + 512, C], zC[:, 512 * i : 512 * i + 512])
-        scatter(zD, D, 0, S)
-        quantise(w2q, w2s, w2g, 0, N)
+        VH = V // 2
+        zp = [reused.tile([P, 2, VH, 2], BF16, name=f"zp{h}", align_bytes=64, offset=20480 + 4096 * h) for h in range(2)]
 
-        zDv = zD[:].rearrange("p (e c) -> p c e", c=512)[:, :, 0:3:2]
-        for i in range(2):
-            vcopy(zg[:, 256 * i : 256 * i + 256, 2:4], zDv[:, 256 * i : 256 * i + 256, :])
-            scopy(zg[:, 512 + 256 * i : 768 + 256 * i, D], zD[:, 512 + 256 * i : 768 + 256 * i])
-        zgf = zg[:].rearrange("p v t -> p (v t)")
+        def gcopy(dst, src):
+            nc.gpsimd.tensor_scalar(dst, src, 1.0, 0.0, MULT, ADD)
 
-        edges = [0, 256, 512, 768, 896, 1024]
-        banks = ["o0", "o1", "o2", "o3", "o4"]
-        for i in range(5):
-            c0, c1 = edges[i], edges[i + 1]
-            quantise(zq, zs, zgf, c0, c1)
-            o = psum.tile([P, c1 - c0], F32, name=f"o{i}", tag=banks[i])
+        def rnd(copy, t, h):
+            copy(zp[h][:, t // 2, :, t % 2], z[t][:, h * VH : (h + 1) * VH])
+
+        def join(copy, c0, c1):
+            h = c0 // VH
+            zg = held.tile([P, (c1 - c0) * 4], BF16, name=f"zg{c0}", align_bytes=64)
+            copy(
+                zg[:].bitcast(U32).rearrange("p (c u) -> p c u", u=2),
+                zp[h][:].rearrange("p u c e -> p (u c e)").bitcast(U32).rearrange("p (u c) -> p c u", u=2)[:, c0 - h * VH : c1 - h * VH],
+            )
+            return zg
+
+        w2g = held.tile([P, N * 4], BF16, name="w2g", tag=f"w1q{D}", align_bytes=64)
+        gcopy(w2g[:].rearrange("p (n j) -> p n j", j=4), w2raw[:].rearrange("p j n -> p n j"))
+        for t, copy in ((A, gcopy), (D, gcopy), (C, vcopy)):
+            for h in range(2):
+                rnd(copy, t, h)
+        w2q = held.tile([P, N], U32, name="w2q", tag=f"hg{C}", align_bytes=64)
+        quantise(w2q[:], w2s[:], w2g, 0, N)
+
+        def layer2(i, c0, c1, zg, g0, copy):
+            quantise(zq[:, c0:c1], zs[:, c0:c1], zg, c0 - g0, c1 - g0)
+            o = psum.tile([P, c1 - c0], F32, name=f"o{i}", tag=f"h{i}")
             nc.tensor.matmul_mx(
                 out=o[:], lhsT=w2q[:].bitcast(FP8X4), lhsT_scale=w2s[:],
                 rhs=zq[:, c0:c1].bitcast(FP8X4), rhs_scale=zs[:, c0:c1], start=True, stop=True,
             )
             res = held.tile([P, c1 - c0], F32, name=f"res{i}")
-            (vcopy if i == 4 else scopy)(res[:], o[:])
+            copy(res[:], o[:])
             nc.sync.dma_start(out[:, c0:c1], res[:])
+
+        rnd(vcopy, B, 1)
+        rnd(vcopy, B, 0)
+        g2 = join(scopy, 512, 768)
+        g3 = join(scopy, 768, V)
+        g0 = join(vcopy, 0, 256)
+        g1 = join(vcopy, 256, 512)
+        layer2(0, 0, 256, g0, 0, scopy)
+        layer2(1, 256, 512, g1, 256, scopy)
+        layer2(2, 512, 768, g2, 512, scopy)
+        layer2(3, 768, 896, g3, 768, scopy)
+        layer2(4, 896, V, g3, 768, vcopy)

@@ -26,6 +26,9 @@ def tile_picked_voxel_relu_e_kernel(tc, xT, w1, w2, gate, offs, pos1, out):
     def acopy(dst, src):
         nc.scalar.activation(dst, src, COPY)
 
+    def gcopy(dst, src):
+        nc.gpsimd.tensor_scalar(dst, src, 1.0, 0.0, MULT, ADD)
+
     with ExitStack() as ctx:
         held = ctx.enter_context(tc.tile_pool(name="held", bufs=1))
         reused = ctx.enter_context(tc.tile_pool(name="reused", bufs=1))
@@ -34,7 +37,7 @@ def tile_picked_voxel_relu_e_kernel(tc, xT, w1, w2, gate, offs, pos1, out):
         points = held.tile([P, S // 16], U16, name="points")
         cells = held.tile([P, S // 16], U16, name="cells")
         gates = held.tile([P, S], F32, name="gates")
-        w2raw = reused.tile([P, 4, N], F32, name="w2raw", align_bytes=64, offset=20480 + 3072)
+        w2raw = reused.tile([P, 5, N], F32, name="w2raw", align_bytes=64, offset=24576 + 2048 - 256)
         xv = xT.rearrange("(p j) w -> p j w", j=4)
         wv = w1.rearrange("(p j) w -> p j w", j=4)
 
@@ -54,9 +57,9 @@ def tile_picked_voxel_relu_e_kernel(tc, xT, w1, w2, gate, offs, pos1, out):
         nc.sync.dma_start(cells[:], pos1)
         w2v = w2.rearrange("(g t r) n -> r g t n", t=4, r=8)
         for r in range(8):
-            nc.sync.dma_start(w2raw[r:P:8, :, :], w2v[r])
+            nc.sync.dma_start(w2raw[r:P:8, 0:4, :], w2v[r])
 
-        A, D, C, B = 0, 1, 2, 3
+        A, C, D, B = 0, 1, 2, 3
         z = [held.tile([P, V], F32, name=f"z{t}") for t in range(4)]
         nc.vector.memset(z[A][:], 0.0)
         nc.gpsimd.memset(z[C][:], 0.0)
@@ -71,7 +74,7 @@ def tile_picked_voxel_relu_e_kernel(tc, xT, w1, w2, gate, offs, pos1, out):
         w1q = {t: held.tile([P, 128], U32, name=f"w1q{t}", align_bytes=64) for t in (B, C, D)}
         w1s = [held.tile([P, 128], U8, name=f"w1s{t}", align_bytes=64) for t in range(4)]
         w2s = held.tile([P, N], U8, name="w2s", align_bytes=64)
-        hg = [held.tile([P, S], F32, name=f"hg{t}", align_bytes=64) for t in range(4)]
+        hg = {t: held.tile([P, S], F32, name=f"hg{t}", align_bytes=64) for t in range(4)}
         zq = held.tile([P, V], U32, name="zq", align_bytes=64)
         zs = held.tile([P, V], U8, name="zs", align_bytes=64)
 
@@ -104,11 +107,17 @@ def tile_picked_voxel_relu_e_kernel(tc, xT, w1, w2, gate, offs, pos1, out):
                 w1raw[:].rearrange("p j (g t r i) -> p t g r j i", t=4, r=2, i=4)[:, t, :, :, j0:j1],
             )
 
+        def gturn(t):
+            gcopy(
+                w1g[t].rearrange("p (g r j) -> p g r j", r=8, j=4)[:, :, :, 0:2],
+                w1raw[:].rearrange("p j (g t r) -> p t g r j", t=4, r=8)[:, t, :, :, 0:2],
+            )
+
         def scatter(copy, t, n0, n1):
             copy(z[t][:].indirect(cells[:, n0 // 16 : n1 // 16]), hg[t][:, n0:n1])
 
-        def layer1(name, t, edges):
-            acc = psum.tile([P, edges[-1] - edges[0]], F32, name=name)
+        def layer1(bank, t, edges):
+            acc = psum.tile([P, edges[-1] - edges[0]], F32, name=f"h{t}_{edges[0]}", tag=bank)
             for n0, n1 in zip(edges, edges[1:]):
                 nc.tensor.matmul_mx(
                     out=acc[:, n0 - edges[0] : n1 - edges[0]], lhsT=w1q[t][:].bitcast(FP8X4),
@@ -131,58 +140,57 @@ def tile_picked_voxel_relu_e_kernel(tc, xT, w1, w2, gate, offs, pos1, out):
         pick(1, 1)
         quantise_x(0)
         quantise_x(1)
-        w1g = {t: reused.tile([P, H], BF16, name=f"w1g{t}", align_bytes=64, offset=at)[:] for t, at in ((A, 12288), (C, 13312), (B, 14336))}
+        w1g = {t: reused.tile([P, H], BF16, name=f"w1g{t}", align_bytes=64, offset=12288 + 1024 * t)[:] for t in range(4)}
         turn(scopy, A, 0, 2)
-        turn(scopy, C, 0, 2)
-        turn(scopy, A, 2, 4)
-        turn(scopy, B)
-        turn(scopy, C, 2, 4)
+        turn(scopy, B, 0, 2)
+        gturn(C)
+        gturn(D)
+        for t in (A, B, C, D):
+            turn(scopy, t, 2, 4)
         w1q[A] = held.tile([P, 128], U32, name="w1qA", tag="xraw0", align_bytes=64)
         quantise_w1(A)
         layer1("h0", A, [0, 128])
         quantise_w1(B)
-        w1g[D] = reused.tile([P, H], BF16, name="w1gD", align_bytes=64, offset=12288)[:]
-        turn(vcopy, D)
         layer1("h1", B, [0, 128])
         scatter(acopy, A, 0, 128)
         scatter(acopy, B, 0, 128)
         quantise_w1(C)
         quantise_w1(D)
+        w2g = reused.tile([P, N * 4], BF16, name="w2g", align_bytes=64, offset=12288 + 1024 * D)
+        gcopy(w2g[:].rearrange("p (n j) -> p n j", j=4), w2raw[:, 0:4, :].rearrange("p j n -> p n j"))
         layer1("h2", A, [128, 256, S])
         scatter(acopy, A, 128, S)
-        layer1("h3", C, [0, S])
-        scatter(acopy, C, 0, 320)
+        layer1("h3", C, [0, 256])
+        layer1("h4", C, [256, S])
+        scatter(vcopy, C, 0, 256)
+        scatter(acopy, C, 256, S)
+        layer1("h3", B, [128, 256, S])
+        scatter(acopy, B, 128, S)
         layer1("h4", D, [0, S])
         scatter(vcopy, D, 0, S)
-        layer1("h5", B, [128, 256, S])
-        scatter(acopy, B, 128, S)
-        scatter(vcopy, C, 320, S)
+        w2q = held.tile([P, N], U32, name="w2q", tag=f"hg{D}", align_bytes=64)
+        quantise(w2q[:], w2s[:], w2g, 0, N)
 
-        VH = V // 2
-        zp = [reused.tile([P, 2, VH, 2], BF16, name=f"zp{h}", align_bytes=64, offset=20480 + 4096 * h) for h in range(2)]
-
-        def gcopy(dst, src):
-            nc.gpsimd.tensor_scalar(dst, src, 1.0, 0.0, MULT, ADD)
+        cuts = [0, 256, 512, V]
+        zp = [
+            reused.tile([P, 2, c1 - c0, 2], BF16, name=f"zp{c0}", align_bytes=64, offset=24576 + 8 * c0)
+            for c0, c1 in zip(cuts, cuts[1:])
+        ]
 
         def rnd(copy, t, h):
-            copy(zp[h][:, t // 2, :, t % 2], z[t][:, h * VH : (h + 1) * VH])
+            copy(zp[h][:, t // 2, :, t % 2], z[t][:, cuts[h] : cuts[h + 1]])
 
-        def join(copy, c0, c1):
-            h = c0 // VH
-            zg = held.tile([P, (c1 - c0) * 4], BF16, name=f"zg{c0}", align_bytes=64)
+        def join(copy, h, c0, c1):
+            zg = reused.tile([P, (c1 - c0) * 4], BF16, name=f"zg{c0}", align_bytes=64, offset=12288 + 1024 * D + 8 * c0)
             copy(
                 zg[:].bitcast(U32).rearrange("p (c u) -> p c u", u=2),
-                zp[h][:].rearrange("p u c e -> p (u c e)").bitcast(U32).rearrange("p (u c) -> p c u", u=2)[:, c0 - h * VH : c1 - h * VH],
+                zp[h][:].rearrange("p u c e -> p (u c e)").bitcast(U32).rearrange("p (u c) -> p c u", u=2)[:, c0 - cuts[h] : c1 - cuts[h]],
             )
             return zg
 
-        w2g = held.tile([P, N * 4], BF16, name="w2g", tag=f"w1q{D}", align_bytes=64)
-        gcopy(w2g[:].rearrange("p (n j) -> p n j", j=4), w2raw[:].rearrange("p j n -> p n j"))
-        for t, copy in ((A, gcopy), (D, gcopy), (C, vcopy)):
-            for h in range(2):
+        for t, copy in ((A, gcopy), (C, gcopy), (D, vcopy)):
+            for h in range(3):
                 rnd(copy, t, h)
-        w2q = held.tile([P, N], U32, name="w2q", tag=f"hg{C}", align_bytes=64)
-        quantise(w2q[:], w2s[:], w2g, 0, N)
 
         def layer2(i, c0, c1, zg, g0, copy):
             quantise(zq[:, c0:c1], zs[:, c0:c1], zg, c0 - g0, c1 - g0)
@@ -195,12 +203,13 @@ def tile_picked_voxel_relu_e_kernel(tc, xT, w1, w2, gate, offs, pos1, out):
             copy(res[:], o[:])
             nc.sync.dma_start(out[:, c0:c1], res[:])
 
-        rnd(vcopy, B, 1)
+        rnd(vcopy, B, 2)
         rnd(vcopy, B, 0)
-        g2 = join(scopy, 512, 768)
-        g3 = join(scopy, 768, V)
-        g0 = join(vcopy, 0, 256)
-        g1 = join(vcopy, 256, 512)
+        rnd(vcopy, B, 1)
+        g2 = join(scopy, 2, 512, 768)
+        g3 = join(scopy, 2, 768, V)
+        g0 = join(vcopy, 0, 0, 256)
+        g1 = join(vcopy, 1, 256, 512)
         layer2(0, 0, 256, g0, 0, scopy)
         layer2(1, 256, 512, g1, 256, scopy)
         layer2(2, 512, 768, g2, 512, scopy)

@@ -37,80 +37,60 @@ def tile_picked_voxel_relu_e_kernel(tc, xT, w1, w2, gate, offs, pos1, out):
         points = held.tile([P, S // 16], U16, name="points")
         cells = held.tile([P, S // 16], U16, name="cells")
         gates = held.tile([P, S], F32, name="gates")
-        w2raw = reused.tile([P, 5, N], F32, name="w2raw", align_bytes=64, offset=24576 + 2048 - 256)
+        w2raw = reused.tile([P, 5, N], F32, name="w2raw", align_bytes=64, offset=11264 - 256)
         xv = xT.rearrange("(p j) w -> p j w", j=4)
         wv = w1.rearrange("(p j) w -> p j w", j=4)
 
-        TH = 576
-        xraw = [
-            [held.tile([P, 2, T], F32, name="xraw0", align_bytes=64)],
-            [reused.tile([P, 2, TH], F32, name="xraw10", align_bytes=64, offset=12288), held.tile([P, 2, T - TH], F32, name="xraw11")],
-        ]
+        xraw = [held.tile([P, T], F32, name=f"xraw{j}") for j in range(4)]
         w1raw = held.tile([P, 4, H], F32, name="w1raw")
-        nc.sync.dma_start(xraw[0][0][:], xv[:, 0:2, :])
+        nc.sync.dma_start(xraw[0][:], xv[:, 0, :])
         nc.sync.dma_start(points[:], offs)
-        nc.sync.dma_start(xraw[1][1][:], xv[:, 2:4, TH:T])
-        nc.sync.dma_start(xraw[1][0][:], xv[:, 2:4, 0:TH])
+        for j in range(1, 4):
+            nc.sync.dma_start(xraw[j][:], xv[:, j, :])
         for b in range(2):
             nc.sync.dma_start(w1raw[:, 2 * b : 2 * b + 2, :], wv[:, 2 * b : 2 * b + 2, :])
         nc.sync.dma_start(gates[:], gate)
         nc.sync.dma_start(cells[:], pos1)
-        w2v = w2.rearrange("(g t r) n -> r g t n", t=4, r=8)
-        for r in range(8):
-            nc.sync.dma_start(w2raw[r:P:8, 0:4, :], w2v[r])
+        w2v = w2.rearrange("(q t i) n -> i q t n", t=4, i=4)
+        for i in range(4):
+            nc.sync.dma_start(w2raw[i:P:4, 0:4, :], w2v[i])
 
         A, C, D, B = 0, 1, 2, 3
         z = [held.tile([P, V], F32, name=f"z{t}") for t in range(4)]
         nc.vector.memset(z[A][:], 0.0)
         nc.gpsimd.memset(z[C][:], 0.0)
-        nc.vector.memset(z[B][:], 0.0)
+        acopy(z[B][:], z[A][:])
         nc.gpsimd.memset(z[D][:], 0.0)
 
-        pairs = [held.tile([P, 2 * T], BF16, name="pairs0", align_bytes=64)[:]]
         SH = S // 2
-        xg = [reused.tile([P, SH * 4], BF16, name=f"xg{a}", align_bytes=64, offset=8192 + 2048 * a) for a in range(2)]
+        xg = [reused.tile([P, SH * 4], BF16, name=f"xg{a}", align_bytes=64, offset=2048 * a) for a in range(2)]
+        xrows = [held.tile([P, 2, SH], BF16, name=f"xrows{u}") for u in range(2)]
         xq = held.tile([P, S], U32, name="xq", align_bytes=64)
         xs = held.tile([P, S], U8, name="xs", align_bytes=64)
-        w1q = {t: held.tile([P, 128], U32, name=f"w1q{t}", align_bytes=64) for t in (B, C, D)}
+        w1q = [held.tile([P, 128], U32, name=f"w1q{t}", align_bytes=64) for t in range(4)]
         w1s = [held.tile([P, 128], U8, name=f"w1s{t}", align_bytes=64) for t in range(4)]
         w2s = held.tile([P, N], U8, name="w2s", align_bytes=64)
         hg = {t: held.tile([P, S], F32, name=f"hg{t}", align_bytes=64) for t in range(4)}
         zq = held.tile([P, V], U32, name="zq", align_bytes=64)
         zs = held.tile([P, V], U8, name="zs", align_bytes=64)
 
-        def pair(copy, u, h, c0, c1):
+        def quantise(codes, scales, grouped):
+            nc.vector.quantize_mx(out=codes.bitcast(FP8X4), scales=scales, in_=grouped)
+
+        def pick(j):
+            vcopy(xg[0][:].rearrange("p (n j) -> p n j", j=4)[:, :, j], xraw[j][:].indirect(points[:, 0 : SH // 16]))
+            acopy(xrows[j // 2][:, j % 2, :], xraw[j][:].indirect(points[:, SH // 16 : S // 16]))
+
+        def weave(copy, u):
             copy(
-                pairs[u].rearrange("p (w e) -> p w e", e=2)[:, h * TH + c0 : h * TH + c1, :],
-                xraw[u][h][:].rearrange("p e w -> p w e")[:, c0:c1, :],
+                xg[1][:].rearrange("p (n j) -> p n j", j=4)[:, :, 2 * u : 2 * u + 2],
+                xrows[u][:].rearrange("p j n -> p n j"),
             )
 
-        def pick(u, a):
-            nc.vector.tensor_copy(
-                xg[a][:].bitcast(U32).rearrange("p (n u) -> p n u", u=2)[:, :, u],
-                pairs[u].bitcast(U32).indirect(points[:, a * SH // 16 : (a + 1) * SH // 16]),
-            )
-
-        def quantise_x(a):
-            quantise(xq[:, a * SH : (a + 1) * SH], xs[:, a * SH : (a + 1) * SH], xg[a], 0, SH)
-
-        def quantise(codes, scales, grouped, c0, c1):
-            nc.vector.quantize_mx(
-                out=codes.bitcast(FP8X4), scales=scales, in_=grouped[:, 4 * c0 : 4 * c1]
-            )
-
-        def quantise_w1(t):
-            quantise(w1q[t][:], w1s[t][:], w1g[t], 0, 128)
-
-        def turn(copy, t, j0=0, j1=4):
+        def turn(copy, t, j0, j1):
             copy(
-                w1g[t].rearrange("p (g r i j) -> p g r j i", r=2, i=4, j=4)[:, :, :, j0:j1],
-                w1raw[:].rearrange("p j (g t r i) -> p t g r j i", t=4, r=2, i=4)[:, t, :, :, j0:j1],
-            )
-
-        def gturn(t):
-            gcopy(
-                w1g[t].rearrange("p (g r j) -> p g r j", r=8, j=4)[:, :, :, 0:2],
-                w1raw[:].rearrange("p j (g t r) -> p t g r j", t=4, r=8)[:, t, :, :, 0:2],
+                w1g[t][:].rearrange("p (q i j) -> p q j i", i=4, j=4)[:, :, j0:j1],
+                w1raw[:].rearrange("p j (q t i) -> p t q j i", t=4, i=4)[:, t, :, j0:j1],
             )
 
         def scatter(copy, t, n0, n1):
@@ -128,35 +108,34 @@ def tile_picked_voxel_relu_e_kernel(tc, xT, w1, w2, gate, offs, pos1, out):
                 hg[t][:, edges[0] : edges[-1]], acc[:], 0.0, gates[:, edges[0] : edges[-1]], MAX, MULT
             )
 
-        pair(vcopy, 0, 0, 0, 704)
-        pair(acopy, 0, 0, 704, T)
-        pick(0, 0)
-        pick(0, 1)
-        pairs.append(held.tile([P, 2 * T], BF16, name="pairs1", tag="xraw0", align_bytes=64)[:])
-        pair(scopy, 1, 1, 0, T - TH)
-        pair(vcopy, 1, 0, 0, 384)
-        pair(scopy, 1, 0, 384, TH)
-        pick(1, 0)
-        pick(1, 1)
-        quantise_x(0)
-        quantise_x(1)
-        w1g = {t: reused.tile([P, H], BF16, name=f"w1g{t}", align_bytes=64, offset=12288 + 1024 * t)[:] for t in range(4)}
+        pick(0)
+        pick(1)
+        weave(scopy, 0)
+        pick(2)
+        pick(3)
+        weave(vcopy, 1)
+        for a in range(2):
+            quantise(xq[:, a * SH : (a + 1) * SH], xs[:, a * SH : (a + 1) * SH], xg[a][:])
+        w1g = {
+            A: held.tile([P, H], BF16, name="w1gA", align_bytes=64),
+            B: held.tile([P, H], BF16, name="w1gB", align_bytes=64),
+            C: reused.tile([P, H], BF16, name="w1gC", align_bytes=64, offset=2048),
+            D: reused.tile([P, H], BF16, name="w1gD", align_bytes=64, offset=4096),
+        }
         turn(scopy, A, 0, 2)
         turn(scopy, B, 0, 2)
-        gturn(C)
-        gturn(D)
-        for t in (A, B, C, D):
-            turn(scopy, t, 2, 4)
-        w1q[A] = held.tile([P, 128], U32, name="w1qA", tag="xraw0", align_bytes=64)
-        quantise_w1(A)
+        turn(vcopy, A, 2, 4)
+        turn(scopy, B, 2, 4)
+        turn(vcopy, C, 0, 4)
+        turn(scopy, D, 0, 4)
+        for t in (A, B, C):
+            quantise(w1q[t][:], w1s[t][:], w1g[t][:])
         layer1("h0", A, [0, 128])
-        quantise_w1(B)
         layer1("h1", B, [0, 128])
         scatter(acopy, A, 0, 128)
         scatter(acopy, B, 0, 128)
-        quantise_w1(C)
-        quantise_w1(D)
-        w2g = reused.tile([P, N * 4], BF16, name="w2g", align_bytes=64, offset=12288 + 1024 * D)
+        quantise(w1q[D][:], w1s[D][:], w1g[D][:])
+        w2g = reused.tile([P, N * 4], BF16, name="w2g", align_bytes=64, offset=4096)
         gcopy(w2g[:].rearrange("p (n j) -> p n j", j=4), w2raw[:, 0:4, :].rearrange("p j n -> p n j"))
         layer1("h2", A, [128, 256, S])
         scatter(acopy, A, 128, S)
@@ -164,36 +143,42 @@ def tile_picked_voxel_relu_e_kernel(tc, xT, w1, w2, gate, offs, pos1, out):
         layer1("h4", C, [256, S])
         scatter(vcopy, C, 0, 256)
         scatter(acopy, C, 256, S)
-        layer1("h3", B, [128, 256, S])
-        scatter(acopy, B, 128, S)
-        layer1("h4", D, [0, S])
+        layer1("h5", D, [0, S])
+        layer1("h6", B, [128, 256, S])
         scatter(vcopy, D, 0, S)
+        scatter(acopy, B, 128, S)
         w2q = held.tile([P, N], U32, name="w2q", tag=f"hg{D}", align_bytes=64)
-        quantise(w2q[:], w2s[:], w2g, 0, N)
+        quantise(w2q[:], w2s[:], w2g[:])
 
-        cuts = [0, 256, 512, V]
+        cuts = [0, 256, 640, V]
         zp = [
-            reused.tile([P, 2, c1 - c0, 2], BF16, name=f"zp{c0}", align_bytes=64, offset=24576 + 8 * c0)
-            for c0, c1 in zip(cuts, cuts[1:])
+            reused.tile([P, 2, c1 - c0, 2], BF16, name=f"zp{c0}", align_bytes=64, offset=(11264, 8192, 13312)[h])
+            for h, (c0, c1) in enumerate(zip(cuts, cuts[1:]))
         ]
 
         def rnd(copy, t, h):
             copy(zp[h][:, t // 2, :, t % 2], z[t][:, cuts[h] : cuts[h + 1]])
 
+        def rnd_both(h):
+            c0, c1 = cuts[h], cuts[h + 1]
+            vcopy(zp[h][:, 1], z[D][:, c0:c1].unsqueeze(2).to_broadcast([P, c1 - c0, 2]))
+
         def join(copy, h, c0, c1):
-            zg = reused.tile([P, (c1 - c0) * 4], BF16, name=f"zg{c0}", align_bytes=64, offset=12288 + 1024 * D + 8 * c0)
+            zg = held.tile([P, (c1 - c0) * 4], BF16, name=f"zg{c0}", align_bytes=64)
             copy(
                 zg[:].bitcast(U32).rearrange("p (c u) -> p c u", u=2),
                 zp[h][:].rearrange("p u c e -> p (u c e)").bitcast(U32).rearrange("p (u c) -> p c u", u=2)[:, c0 - cuts[h] : c1 - cuts[h]],
             )
             return zg
 
-        for t, copy in ((A, gcopy), (C, gcopy), (D, vcopy)):
+        for t in (A, C):
             for h in range(3):
-                rnd(copy, t, h)
+                rnd(gcopy, t, h)
+        for h in (2, 0, 1):
+            rnd_both(h)
 
-        def layer2(i, c0, c1, zg, g0, copy):
-            quantise(zq[:, c0:c1], zs[:, c0:c1], zg, c0 - g0, c1 - g0)
+        def layer2(i, c0, c1, zg, copy):
+            quantise(zq[:, c0:c1], zs[:, c0:c1], zg[:])
             o = psum.tile([P, c1 - c0], F32, name=f"o{i}", tag=f"h{i}")
             nc.tensor.matmul_mx(
                 out=o[:], lhsT=w2q[:].bitcast(FP8X4), lhsT_scale=w2s[:],
@@ -203,15 +188,16 @@ def tile_picked_voxel_relu_e_kernel(tc, xT, w1, w2, gate, offs, pos1, out):
             copy(res[:], o[:])
             nc.sync.dma_start(out[:, c0:c1], res[:])
 
-        rnd(vcopy, B, 2)
         rnd(vcopy, B, 0)
         rnd(vcopy, B, 1)
-        g2 = join(scopy, 2, 512, 768)
-        g3 = join(scopy, 2, 768, V)
+        rnd(scopy, B, 2)
+        g3 = join(scopy, 2, 640, 896)
+        g4 = join(scopy, 2, 896, V)
         g0 = join(vcopy, 0, 0, 256)
         g1 = join(vcopy, 1, 256, 512)
-        layer2(0, 0, 256, g0, 0, scopy)
-        layer2(1, 256, 512, g1, 256, scopy)
-        layer2(2, 512, 768, g2, 512, scopy)
-        layer2(3, 768, 896, g3, 768, scopy)
-        layer2(4, 896, V, g3, 768, vcopy)
+        layer2(0, 0, 256, g0, scopy)
+        g2 = join(vcopy, 1, 512, 640)
+        layer2(1, 256, 512, g1, scopy)
+        layer2(2, 640, 896, g3, scopy)
+        layer2(3, 512, 640, g2, scopy)
+        layer2(4, 896, V, g4, vcopy)

@@ -36,7 +36,7 @@ def tile_picked_voxel_relu_e_kernel(tc, xT, w1, w2, gate, offs, pos1, out):
 
         points = held.tile([P, S // 16], U16, name="points")
         cells = held.tile([P, S // 16], U16, name="cells")
-        gates = held.tile([P, S], F32, name="gates")
+        gates = reused.tile([P, S], F32, name="gates", align_bytes=64, offset=6144)
         w2raw = reused.tile([P, 5, N], F32, name="w2raw", align_bytes=64, offset=11264 - 256)
         xv = xT.rearrange("(p j) w -> p j w", j=4)
         wv = w1.rearrange("(p j) w -> p j w", j=4)
@@ -139,43 +139,33 @@ def tile_picked_voxel_relu_e_kernel(tc, xT, w1, w2, gate, offs, pos1, out):
         gcopy(w2g[:].rearrange("p (n j) -> p n j", j=4), w2raw[:, 0:4, :].rearrange("p j n -> p n j"))
         layer1("h2", A, [128, 256, S])
         scatter(acopy, A, 128, S)
-        layer1("h3", C, [0, 256])
-        layer1("h4", C, [256, S])
-        scatter(vcopy, C, 0, 256)
-        scatter(acopy, C, 256, S)
+        layer1("h3", C, [0, S])
+        scatter(vcopy, C, 0, 320)
+        scatter(acopy, C, 320, S)
         layer1("h5", D, [0, S])
         layer1("h6", B, [128, 256, S])
         scatter(vcopy, D, 0, S)
         scatter(acopy, B, 128, S)
-        w2q = held.tile([P, N], U32, name="w2q", tag=f"hg{D}", align_bytes=64)
+        w2q = reused.tile([P, N], U32, name="w2q", align_bytes=64, offset=6144)
         quantise(w2q[:], w2s[:], w2g[:])
 
-        cuts = [0, 256, 640, V]
-        zp = [
-            reused.tile([P, 2, c1 - c0, 2], BF16, name=f"zp{c0}", align_bytes=64, offset=(11264, 8192, 13312)[h])
-            for h, (c0, c1) in enumerate(zip(cuts, cuts[1:]))
-        ]
+        zp = reused.tile([P, 2, V, 2], BF16, name="zp", align_bytes=64, offset=8192)
 
-        def rnd(copy, t, h):
-            copy(zp[h][:, t // 2, :, t % 2], z[t][:, cuts[h] : cuts[h + 1]])
+        def rnd(copy, t, c0, c1):
+            copy(zp[:, t // 2, c0:c1, t % 2], z[t][:, c0:c1])
 
-        def rnd_both(h):
-            c0, c1 = cuts[h], cuts[h + 1]
-            vcopy(zp[h][:, 1], z[D][:, c0:c1].unsqueeze(2).to_broadcast([P, c1 - c0, 2]))
-
-        def join(copy, h, c0, c1):
+        def join(copy, c0, c1):
             zg = held.tile([P, (c1 - c0) * 4], BF16, name=f"zg{c0}", align_bytes=64)
             copy(
                 zg[:].bitcast(U32).rearrange("p (c u) -> p c u", u=2),
-                zp[h][:].rearrange("p u c e -> p (u c e)").bitcast(U32).rearrange("p (u c) -> p c u", u=2)[:, c0 - cuts[h] : c1 - cuts[h]],
+                zp[:].rearrange("p u c e -> p (u c e)").bitcast(U32).rearrange("p (u c) -> p c u", u=2)[:, c0:c1],
             )
             return zg
 
         for t in (A, C):
-            for h in range(3):
-                rnd(gcopy, t, h)
-        for h in (2, 0, 1):
-            rnd_both(h)
+            rnd(gcopy, t, 0, V)
+        rnd(vcopy, D, 0, 640)
+        rnd(scopy, D, 640, V)
 
         def layer2(i, c0, c1, zg, copy):
             quantise(zq[:, c0:c1], zs[:, c0:c1], zg[:])
@@ -188,16 +178,17 @@ def tile_picked_voxel_relu_e_kernel(tc, xT, w1, w2, gate, offs, pos1, out):
             copy(res[:], o[:])
             nc.sync.dma_start(out[:, c0:c1], res[:])
 
-        rnd(vcopy, B, 0)
-        rnd(vcopy, B, 1)
-        rnd(scopy, B, 2)
-        g3 = join(scopy, 2, 640, 896)
-        g4 = join(scopy, 2, 896, V)
-        g0 = join(vcopy, 0, 0, 256)
-        g1 = join(vcopy, 1, 256, 512)
+        rnd(vcopy, B, 0, 256)
+        rnd(vcopy, B, 256, 640)
+        rnd(scopy, B, 640, 896)
+        rnd(scopy, B, 896, V)
+        g3 = join(scopy, 640, 896)
+        g4 = join(scopy, 896, V)
+        g0 = join(vcopy, 0, 256)
+        g1 = join(vcopy, 256, 512)
         layer2(0, 0, 256, g0, scopy)
-        g2 = join(vcopy, 1, 512, 640)
+        g2 = join(vcopy, 512, 640)
         layer2(1, 256, 512, g1, scopy)
         layer2(2, 640, 896, g3, scopy)
-        layer2(3, 512, 640, g2, scopy)
+        layer2(3, 512, 640, g2, vcopy)
         layer2(4, 896, V, g4, vcopy)

@@ -120,7 +120,7 @@ def tile_picked_voxel_relu_e_kernel(tc, xT, w1, w2, gate, offs, pos1, out):
             A: held.tile([P, H], BF16, name="w1gA", align_bytes=64),
             B: held.tile([P, H], BF16, name="w1gB", align_bytes=64),
             C: reused.tile([P, H], BF16, name="w1gC", align_bytes=64, offset=2048),
-            D: reused.tile([P, H], BF16, name="w1gD", align_bytes=64, offset=4096),
+            D: held.tile([P, H], BF16, name="w1gD", align_bytes=64),
         }
         turn(scopy, A, 0, 2)
         turn(scopy, B, 0, 2)
@@ -135,21 +135,21 @@ def tile_picked_voxel_relu_e_kernel(tc, xT, w1, w2, gate, offs, pos1, out):
         scatter(acopy, A, 0, 128)
         scatter(acopy, B, 0, 128)
         quantise(w1q[D][:], w1s[D][:], w1g[D][:])
-        w2g = reused.tile([P, N * 4], BF16, name="w2g", align_bytes=64, offset=4096)
-        gcopy(w2g[:].rearrange("p (n j) -> p n j", j=4), w2raw[:, 0:4, :].rearrange("p j n -> p n j"))
         layer1("h2", A, [128, 256, S])
         scatter(acopy, A, 128, S)
         layer1("h3", C, [0, S])
-        scatter(vcopy, C, 0, 320)
-        scatter(acopy, C, 320, S)
         layer1("h5", D, [0, S])
         layer1("h6", B, [128, 256, S])
-        scatter(vcopy, D, 0, S)
+        w2g = reused.tile([P, N * 4], BF16, name="w2g", align_bytes=64, offset=6144 + 512)
+        gcopy(w2g[:].rearrange("p (n j) -> p n j", j=4), w2raw[:, 0:4, :].rearrange("p j n -> p n j"))
+        scatter(vcopy, C, 0, S)
+        scatter(acopy, D, 320, S)
+        scatter(vcopy, D, 0, 320)
         scatter(acopy, B, 128, S)
         w2q = reused.tile([P, N], U32, name="w2q", align_bytes=64, offset=6144)
         quantise(w2q[:], w2s[:], w2g[:])
 
-        zp = reused.tile([P, 2, V, 2], BF16, name="zp", align_bytes=64, offset=8192)
+        zp = reused.tile([P, 2, V, 2], BF16, name="zp", align_bytes=64, offset=8192 - 256)
 
         def rnd(copy, t, c0, c1):
             copy(zp[:, t // 2, c0:c1, t % 2], z[t][:, c0:c1])

@@ -37,7 +37,7 @@ def tile_picked_voxel_relu_e_kernel(tc, xT, w1, w2, gate, offs, pos1, out):
         points = held.tile([P, S // 16], U16, name="points")
         cells = held.tile([P, S // 16], U16, name="cells")
         gates = reused.tile([P, S], F32, name="gates", align_bytes=64, offset=6144)
-        w2raw = reused.tile([P, 5, N], F32, name="w2raw", align_bytes=64, offset=11264 - 256)
+        w2raw = held.tile([P, 4, N], F32, name="w2raw", align_bytes=64)
         xv = xT.rearrange("(p j) w -> p j w", j=4)
         wv = w1.rearrange("(p j) w -> p j w", j=4)
 
@@ -118,33 +118,33 @@ def tile_picked_voxel_relu_e_kernel(tc, xT, w1, w2, gate, offs, pos1, out):
             quantise(xq[:, a * SH : (a + 1) * SH], xs[:, a * SH : (a + 1) * SH], xg[a][:])
         w1g = {
             A: held.tile([P, H], BF16, name="w1gA", align_bytes=64),
-            B: held.tile([P, H], BF16, name="w1gB", align_bytes=64),
-            C: reused.tile([P, H], BF16, name="w1gC", align_bytes=64, offset=2048),
-            D: held.tile([P, H], BF16, name="w1gD", align_bytes=64),
+            C: held.tile([P, H], BF16, name="w1gC", align_bytes=64),
+            B: reused.tile([P, H], BF16, name="w1gB", align_bytes=64, offset=2048),
+            D: reused.tile([P, H], BF16, name="w1gD", align_bytes=64, offset=4096),
         }
         turn(scopy, A, 0, 2)
-        turn(scopy, B, 0, 2)
+        turn(scopy, C, 0, 2)
         turn(vcopy, A, 2, 4)
-        turn(scopy, B, 2, 4)
-        turn(vcopy, C, 0, 4)
+        turn(scopy, C, 2, 4)
+        turn(vcopy, B, 0, 4)
         turn(scopy, D, 0, 4)
-        for t in (A, B, C):
+        for t in (A, C, B):
             quantise(w1q[t][:], w1s[t][:], w1g[t][:])
         layer1("h0", A, [0, 128])
-        layer1("h1", B, [0, 128])
+        layer1("h1", C, [0, 128])
         scatter(acopy, A, 0, 128)
-        scatter(acopy, B, 0, 128)
+        scatter(acopy, C, 0, 128)
         quantise(w1q[D][:], w1s[D][:], w1g[D][:])
         layer1("h2", A, [128, 256, S])
         scatter(acopy, A, 128, S)
-        layer1("h3", C, [0, S])
+        layer1("h3", B, [0, S])
         layer1("h5", D, [0, S])
-        layer1("h6", B, [128, 256, S])
-        w2g = reused.tile([P, N * 4], BF16, name="w2g", align_bytes=64, offset=6144 + 512)
+        layer1("h6", C, [128, 256, S])
+        w2g = reused.tile([P, N * 4], BF16, name="w2g", align_bytes=64, offset=4096)
         gcopy(w2g[:].rearrange("p (n j) -> p n j", j=4), w2raw[:, 0:4, :].rearrange("p j n -> p n j"))
-        scatter(vcopy, C, 0, S)
-        scatter(acopy, D, 320, S)
-        scatter(vcopy, D, 0, 320)
+        scatter(vcopy, B, 0, 128)
+        scatter(vcopy, D, 0, S)
+        scatter(acopy, C, 128, S)
         scatter(acopy, B, 128, S)
         w2q = reused.tile([P, N], U32, name="w2q", align_bytes=64, offset=6144)
         quantise(w2q[:], w2s[:], w2g[:])
@@ -162,10 +162,10 @@ def tile_picked_voxel_relu_e_kernel(tc, xT, w1, w2, gate, offs, pos1, out):
             )
             return zg
 
-        for t in (A, C):
-            rnd(gcopy, t, 0, V)
+        rnd(vcopy, A, 0, V)
+        vcopy(zp[:, 1, 640:V], z[D][:, 640:V].unsqueeze(2).to_broadcast([P, 384, 2]))
         rnd(vcopy, D, 0, 640)
-        rnd(scopy, D, 640, V)
+        rnd(vcopy, C, 0, V)
 
         def layer2(i, c0, c1, zg, copy):
             quantise(zq[:, c0:c1], zs[:, c0:c1], zg[:])
@@ -190,5 +190,5 @@ def tile_picked_voxel_relu_e_kernel(tc, xT, w1, w2, gate, offs, pos1, out):
         g2 = join(vcopy, 512, 640)
         layer2(1, 256, 512, g1, scopy)
         layer2(2, 640, 896, g3, scopy)
-        layer2(3, 512, 640, g2, vcopy)
+        layer2(3, 512, 640, g2, scopy)
         layer2(4, 896, V, g4, vcopy)

@@ -14,7 +14,6 @@ FP8X4 = mybir.dt.float8_e4m3fn_x4
 COPY = mybir.ActivationFunctionType.Copy
 MULT = mybir.AluOpType.mult
 MAX = mybir.AluOpType.max
-ADD = mybir.AluOpType.add
 
 FLOPS = 2 * H * K * S + 2 * N * H * V
 
@@ -25,9 +24,6 @@ def tile_picked_voxel_relu_e_kernel(tc, xT, w1, w2, gate, offs, pos1, out):
 
     def acopy(dst, src):
         nc.scalar.activation(dst, src, COPY)
-
-    def gcopy(dst, src):
-        nc.gpsimd.tensor_scalar(dst, src, 1.0, 0.0, MULT, ADD)
 
     with ExitStack() as ctx:
         held = ctx.enter_context(tc.tile_pool(name="held", bufs=1))
@@ -49,11 +45,11 @@ def tile_picked_voxel_relu_e_kernel(tc, xT, w1, w2, gate, offs, pos1, out):
             nc.sync.dma_start(xraw[j][:], xv[:, j, :])
         for b in range(2):
             nc.sync.dma_start(w1raw[:, 2 * b : 2 * b + 2, :], wv[:, 2 * b : 2 * b + 2, :])
-        nc.sync.dma_start(gates[:], gate)
-        nc.sync.dma_start(cells[:], pos1)
         w2v = w2.rearrange("(q t i) n -> i q t n", t=4, i=4)
         for i in range(4):
-            nc.sync.dma_start(w2raw[i:P:4, 0:4, :], w2v[i])
+            nc.sync.dma_start(w2raw[i:P:4], w2v[i])
+        nc.sync.dma_start(gates[:], gate)
+        nc.sync.dma_start(cells[:], pos1)
 
         A, C, D, B = 0, 1, 2, 3
         z = [held.tile([P, V], F32, name=f"z{t}") for t in range(4)]
@@ -120,7 +116,7 @@ def tile_picked_voxel_relu_e_kernel(tc, xT, w1, w2, gate, offs, pos1, out):
             A: held.tile([P, H], BF16, name="w1gA", align_bytes=64),
             C: held.tile([P, H], BF16, name="w1gC", align_bytes=64),
             B: reused.tile([P, H], BF16, name="w1gB", align_bytes=64, offset=2048),
-            D: reused.tile([P, H], BF16, name="w1gD", align_bytes=64, offset=4096),
+            D: held.tile([P, H], BF16, name="w1gD", align_bytes=64),
         }
         turn(scopy, A, 0, 2)
         turn(scopy, C, 0, 2)
@@ -128,6 +124,8 @@ def tile_picked_voxel_relu_e_kernel(tc, xT, w1, w2, gate, offs, pos1, out):
         turn(scopy, C, 2, 4)
         turn(vcopy, B, 0, 4)
         turn(scopy, D, 0, 4)
+        w2g = held.tile([P, N * 4], BF16, name="w2g", align_bytes=64)
+        scopy(w2g[:].rearrange("p (n i j) -> p n j i", i=4, j=4), w2raw[:].rearrange("p j (n i) -> p n j i", i=4))
         for t in (A, C, B):
             quantise(w1q[t][:], w1s[t][:], w1g[t][:])
         layer1("h0", A, [0, 128])
@@ -140,14 +138,11 @@ def tile_picked_voxel_relu_e_kernel(tc, xT, w1, w2, gate, offs, pos1, out):
         layer1("h3", B, [0, S])
         layer1("h5", D, [0, S])
         layer1("h6", C, [128, 256, S])
-        w2g = reused.tile([P, N * 4], BF16, name="w2g", align_bytes=64, offset=4096)
-        gcopy(w2g[:].rearrange("p (n j) -> p n j", j=4), w2raw[:, 0:4, :].rearrange("p j n -> p n j"))
         scatter(vcopy, B, 0, 128)
         scatter(vcopy, D, 0, S)
         scatter(acopy, C, 128, S)
         scatter(acopy, B, 128, S)
         w2q = reused.tile([P, N], U32, name="w2q", align_bytes=64, offset=6144)
-        quantise(w2q[:], w2s[:], w2g[:])
 
         zp = reused.tile([P, 2, V, 2], BF16, name="zp", align_bytes=64, offset=8192 - 256)
 
@@ -163,6 +158,7 @@ def tile_picked_voxel_relu_e_kernel(tc, xT, w1, w2, gate, offs, pos1, out):
             return zg
 
         rnd(vcopy, A, 0, V)
+        quantise(w2q[:], w2s[:], w2g[:])
         vcopy(zp[:, 1, 640:V], z[D][:, 640:V].unsqueeze(2).to_broadcast([P, 384, 2]))
         rnd(vcopy, D, 0, 640)
         rnd(vcopy, C, 0, V)

@@ -59,7 +59,8 @@ def tile_picked_voxel_relu_e_kernel(tc, xT, w1, w2, gate, offs, pos1, out):
         nc.gpsimd.memset(z[D][:], 0.0)
 
         SH = S // 2
-        xg = [reused.tile([P, SH * 4], BF16, name=f"xg{a}", align_bytes=64, offset=2048 * a) for a in range(2)]
+        xg = reused.tile([P, S * 4], BF16, name="xg", align_bytes=64, offset=0)
+        xslots = xg[:].rearrange("p (n j) -> p n j", j=4)
         xrows = [held.tile([P, 2, SH], BF16, name=f"xrows{u}") for u in range(2)]
         xq = held.tile([P, S], U32, name="xq", align_bytes=64)
         xs = held.tile([P, S], U8, name="xs", align_bytes=64)
@@ -74,14 +75,11 @@ def tile_picked_voxel_relu_e_kernel(tc, xT, w1, w2, gate, offs, pos1, out):
             nc.vector.quantize_mx(out=codes.bitcast(FP8X4), scales=scales, in_=grouped)
 
         def pick(j):
-            vcopy(xg[0][:].rearrange("p (n j) -> p n j", j=4)[:, :, j], xraw[j][:].indirect(points[:, 0 : SH // 16]))
+            vcopy(xslots[:, 0:SH, j], xraw[j][:].indirect(points[:, 0 : SH // 16]))
             acopy(xrows[j // 2][:, j % 2, :], xraw[j][:].indirect(points[:, SH // 16 : S // 16]))
 
-        def weave(copy, u):
-            copy(
-                xg[1][:].rearrange("p (n j) -> p n j", j=4)[:, :, 2 * u : 2 * u + 2],
-                xrows[u][:].rearrange("p j n -> p n j"),
-            )
+        def weave(copy, u, n0, n1):
+            copy(xslots[:, n0:n1, 2 * u : 2 * u + 2], xrows[u][:].rearrange("p j n -> p n j")[:, n0 - SH : n1 - SH])
 
         def turn(copy, t, j0, j1):
             copy(
@@ -106,12 +104,13 @@ def tile_picked_voxel_relu_e_kernel(tc, xT, w1, w2, gate, offs, pos1, out):
 
         pick(0)
         pick(1)
-        weave(scopy, 0)
+        weave(vcopy, 0, SH, S)
         pick(2)
         pick(3)
-        weave(vcopy, 1)
-        for a in range(2):
-            quantise(xq[:, a * SH : (a + 1) * SH], xs[:, a * SH : (a + 1) * SH], xg[a][:])
+        weave(vcopy, 1, SH, 384)
+        weave(vcopy, 1, 384, S)
+        for n0, n1 in ((0, 384), (384, S)):
+            quantise(xq[:, n0:n1], xs[:, n0:n1], xg[:, 4 * n0 : 4 * n1])
         w1g = {
             A: held.tile([P, H], BF16, name="w1gA", align_bytes=64),
             C: held.tile([P, H], BF16, name="w1gC", align_bytes=64),
@@ -138,10 +137,10 @@ def tile_picked_voxel_relu_e_kernel(tc, xT, w1, w2, gate, offs, pos1, out):
         layer1("h3", B, [0, S])
         layer1("h5", D, [0, S])
         layer1("h6", C, [128, 256, S])
-        scatter(vcopy, B, 0, 128)
+        scatter(vcopy, B, 0, 160)
         scatter(vcopy, D, 0, S)
         scatter(acopy, C, 128, S)
-        scatter(acopy, B, 128, S)
+        scatter(acopy, B, 160, S)
         w2q = reused.tile([P, N], U32, name="w2q", align_bytes=64, offset=6144)
 
         zp = reused.tile([P, 2, V, 2], BF16, name="zp", align_bytes=64, offset=8192 - 256)

@@ -158,9 +158,11 @@ def tile_picked_voxel_relu_e_kernel(tc, xT, w1, w2, gate, offs, pos1, out):
 
         rnd(vcopy, A, 0, V)
         quantise(w2q[:], w2s[:], w2g[:])
-        vcopy(zp[:, 1, 640:V], z[D][:, 640:V].unsqueeze(2).to_broadcast([P, 384, 2]))
-        rnd(vcopy, D, 0, 640)
+        vcopy(zp[:, 1, 512:V], z[D][:, 512:V].unsqueeze(2).to_broadcast([P, 512, 2]))
+        rnd(vcopy, D, 0, 512)
         rnd(vcopy, C, 0, V)
+
+        res = [held.tile([P, 256], F32, name=f"res{i}") for i in range(4)]
 
         def layer2(i, c0, c1, zg, copy):
             quantise(zq[:, c0:c1], zs[:, c0:c1], zg[:])
@@ -169,21 +171,21 @@ def tile_picked_voxel_relu_e_kernel(tc, xT, w1, w2, gate, offs, pos1, out):
                 out=o[:], lhsT=w2q[:].bitcast(FP8X4), lhsT_scale=w2s[:],
                 rhs=zq[:, c0:c1].bitcast(FP8X4), rhs_scale=zs[:, c0:c1], start=True, stop=True,
             )
-            res = held.tile([P, c1 - c0], F32, name=f"res{i}")
-            copy(res[:], o[:])
-            nc.sync.dma_start(out[:, c0:c1], res[:])
+            copy(res[c0 // 256][:, c0 % 256 : c0 % 256 + c1 - c0], o[:])
+            if c1 % 256 == 0:
+                nc.sync.dma_start(out[:, c1 - 256 : c1], res[c0 // 256][:])
 
         rnd(vcopy, B, 0, 256)
-        rnd(vcopy, B, 256, 640)
-        rnd(scopy, B, 640, 896)
-        rnd(scopy, B, 896, V)
-        g3 = join(scopy, 640, 896)
+        rnd(vcopy, B, 256, 512)
+        rnd(scopy, B, 512, 768)
+        rnd(scopy, B, 768, V)
+        g2 = join(scopy, 512, 768)
+        g3 = join(scopy, 768, 896)
         g4 = join(scopy, 896, V)
         g0 = join(vcopy, 0, 256)
         g1 = join(vcopy, 256, 512)
         layer2(0, 0, 256, g0, scopy)
-        g2 = join(vcopy, 512, 640)
         layer2(1, 256, 512, g1, scopy)
-        layer2(2, 640, 896, g3, scopy)
-        layer2(3, 512, 640, g2, scopy)
+        layer2(2, 512, 768, g2, scopy)
+        layer2(3, 768, 896, g3, vcopy)
         layer2(4, 896, V, g4, vcopy)

@@ -158,8 +158,10 @@ def tile_picked_voxel_relu_e_kernel(tc, xT, w1, w2, gate, offs, pos1, out):
 
         rnd(vcopy, A, 0, V)
         quantise(w2q[:], w2s[:], w2g[:])
-        vcopy(zp[:, 1, 512:V], z[D][:, 512:V].unsqueeze(2).to_broadcast([P, 512, 2]))
-        rnd(vcopy, D, 0, 512)
+        zp_d = zp[:, 1].rearrange("p (b c) e -> p b c e", c=256)
+        z_d = z[D][:].rearrange("p (b c) -> p b c", c=256)
+        vcopy(zp_d[:, :, 1:256, 0], z_d[:, :, 1:256])
+        vcopy(zp_d[:, :, 0, :], z_d[:, :, 0:1].to_broadcast([P, 4, 2]))
         rnd(vcopy, C, 0, V)
 
         res = [held.tile([P, 256], F32, name=f"res{i}") for i in range(4)]

@@ -166,14 +166,15 @@ def tile_picked_voxel_relu_e_kernel(tc, xT, w1, w2, gate, offs, pos1, out):
 
         res = [held.tile([P, 256], F32, name=f"res{i}") for i in range(4)]
 
-        def layer2(i, c0, c1, zg, copy):
+        def layer2(c0, c1, zg, copies):
             quantise(zq[:, c0:c1], zs[:, c0:c1], zg[:])
-            o = psum.tile([P, c1 - c0], F32, name=f"o{i}", tag=f"h{i}")
-            nc.tensor.matmul_mx(
-                out=o[:], lhsT=w2q[:].bitcast(FP8X4), lhsT_scale=w2s[:],
-                rhs=zq[:, c0:c1].bitcast(FP8X4), rhs_scale=zs[:, c0:c1], start=True, stop=True,
-            )
-            copy(res[c0 // 256][:, c0 % 256 : c0 % 256 + c1 - c0], o[:])
+            for c, copy in zip(range(c0, c1, 128), copies):
+                o = psum.tile([P, 128], F32, name=f"o{c}", tag=f"h{c // 128}")
+                nc.tensor.matmul_mx(
+                    out=o[:], lhsT=w2q[:].bitcast(FP8X4), lhsT_scale=w2s[:],
+                    rhs=zq[:, c : c + 128].bitcast(FP8X4), rhs_scale=zs[:, c : c + 128], start=True, stop=True,
+                )
+                copy(res[c // 256][:, c % 256 : c % 256 + 128], o[:])
             if c1 % 256 == 0:
                 nc.sync.dma_start(out[:, c1 - 256 : c1], res[c0 // 256][:])
 
@@ -186,8 +187,8 @@ def tile_picked_voxel_relu_e_kernel(tc, xT, w1, w2, gate, offs, pos1, out):
         g4 = join(scopy, 896, V)
         g0 = join(vcopy, 0, 256)
         g1 = join(vcopy, 256, 512)
-        layer2(0, 0, 256, g0, scopy)
-        layer2(1, 256, 512, g1, scopy)
-        layer2(2, 512, 768, g2, scopy)
-        layer2(3, 768, 896, g3, vcopy)
-        layer2(4, 896, V, g4, vcopy)
+        layer2(0, 256, g0, [scopy, scopy])
+        layer2(256, 512, g1, [scopy, scopy])
+        layer2(512, 768, g2, [scopy, vcopy])
+        layer2(768, 896, g3, [vcopy])
+        layer2(896, V, g4, [scopy])

@@ -45,9 +45,9 @@ def tile_picked_voxel_relu_e_kernel(tc, xT, w1, w2, gate, offs, pos1, out):
             nc.sync.dma_start(xraw[j][:], xv[:, j, :])
         for b in range(2):
             nc.sync.dma_start(w1raw[:, 2 * b : 2 * b + 2, :], wv[:, 2 * b : 2 * b + 2, :])
-        w2v = w2.rearrange("(q t i) n -> i q t n", t=4, i=4)
-        for i in range(4):
-            nc.sync.dma_start(w2raw[i:P:4], w2v[i])
+        w2v = w2.rearrange("(q t i) n -> i q t n", t=4, i=2)
+        for i in range(2):
+            nc.sync.dma_start(w2raw[i:P:2], w2v[i])
         nc.sync.dma_start(gates[:], gate)
         nc.sync.dma_start(cells[:], pos1)
 
@@ -83,8 +83,8 @@ def tile_picked_voxel_relu_e_kernel(tc, xT, w1, w2, gate, offs, pos1, out):
 
         def turn(copy, t, j0, j1):
             copy(
-                w1g[t][:].rearrange("p (q i j) -> p q j i", i=4, j=4)[:, :, j0:j1],
-                w1raw[:].rearrange("p j (q t i) -> p t q j i", t=4, i=4)[:, t, :, j0:j1],
+                w1g[t][:].rearrange("p (q i j) -> p q j i", i=2, j=4)[:, :, j0:j1],
+                w1raw[:].rearrange("p j (q t i) -> p t q j i", t=4, i=2)[:, t, :, j0:j1],
             )
 
         def scatter(copy, t, n0, n1):

@@ -53,9 +53,9 @@ def tile_picked_voxel_relu_e_kernel(tc, xT, w1, w2, gate, offs, pos1, out):
 
         A, C, D, B = 0, 1, 2, 3
         z = [held.tile([P, V], F32, name=f"z{t}") for t in range(4)]
-        nc.vector.memset(z[A][:], 0.0)
         nc.gpsimd.memset(z[C][:], 0.0)
-        acopy(z[B][:], z[A][:])
+        acopy(z[A][:], z[C][:])
+        nc.gpsimd.memset(z[B][:], 0.0)
         nc.gpsimd.memset(z[D][:], 0.0)
 
         SH = S // 2
@@ -166,17 +166,16 @@ def tile_picked_voxel_relu_e_kernel(tc, xT, w1, w2, gate, offs, pos1, out):
 
         res = [held.tile([P, 256], F32, name=f"res{i}") for i in range(4)]
 
-        def layer2(c0, c1, zg, copies):
+        banks = {}
+
+        def layer2(c0, c1, zg):
             quantise(zq[:, c0:c1], zs[:, c0:c1], zg[:])
-            for c, copy in zip(range(c0, c1, 128), copies):
-                o = psum.tile([P, 128], F32, name=f"o{c}", tag=f"h{c // 128}")
+            for c in range(c0, c1, 128):
+                banks[c] = psum.tile([P, 128], F32, name=f"o{c}", tag=f"h{c // 128}")
                 nc.tensor.matmul_mx(
-                    out=o[:], lhsT=w2q[:].bitcast(FP8X4), lhsT_scale=w2s[:],
+                    out=banks[c][:], lhsT=w2q[:].bitcast(FP8X4), lhsT_scale=w2s[:],
                     rhs=zq[:, c : c + 128].bitcast(FP8X4), rhs_scale=zs[:, c : c + 128], start=True, stop=True,
                 )
-                copy(res[c // 256][:, c % 256 : c % 256 + 128], o[:])
-            if c1 % 256 == 0:
-                nc.sync.dma_start(out[:, c1 - 256 : c1], res[c0 // 256][:])
 
         rnd(vcopy, B, 0, 256)
         rnd(vcopy, B, 256, 512)
@@ -187,8 +186,15 @@ def tile_picked_voxel_relu_e_kernel(tc, xT, w1, w2, gate, offs, pos1, out):
         g4 = join(scopy, 896, V)
         g0 = join(vcopy, 0, 256)
         g1 = join(vcopy, 256, 512)
-        layer2(0, 256, g0, [scopy, scopy])
-        layer2(256, 512, g1, [scopy, scopy])
-        layer2(512, 768, g2, [scopy, vcopy])
-        layer2(768, 896, g3, [vcopy])
-        layer2(896, V, g4, [scopy])
+        layer2(0, 256, g0)
+        layer2(256, 512, g1)
+        layer2(512, 768, g2)
+        layer2(768, 896, g3)
+        layer2(896, V, g4)
+        for c in range(0, V, 128):
+            copy = vcopy if c >= 384 and c % 256 else scopy
+            copy(res[c // 256][:, c % 256 : c % 256 + 128], banks[c][:])
+            if c < 256:
+                nc.sync.dma_start(out[:, c : c + 128], res[0][:, c : c + 128])
+            elif c % 256:
+                nc.sync.dma_start(out[:, c - 128 : c + 128], res[c // 256][:])

@@ -51,7 +51,7 @@ def tile_picked_voxel_relu_e_kernel(tc, xT, w1, w2, gate, offs, pos1, out):
         nc.sync.dma_start(gates[:], gate)
         nc.sync.dma_start(cells[:], pos1)
 
-        A, C, D, B = 0, 1, 2, 3
+        A, B, C, D = 0, 1, 2, 3
         z = [held.tile([P, V], F32, name=f"z{t}") for t in range(4)]
         nc.gpsimd.memset(z[C][:], 0.0)
         acopy(z[A][:], z[C][:])
@@ -114,33 +114,29 @@ def tile_picked_voxel_relu_e_kernel(tc, xT, w1, w2, gate, offs, pos1, out):
         w1g = {
             A: held.tile([P, H], BF16, name="w1gA", align_bytes=64),
             C: held.tile([P, H], BF16, name="w1gC", align_bytes=64),
-            B: reused.tile([P, H], BF16, name="w1gB", align_bytes=64, offset=2048),
-            D: held.tile([P, H], BF16, name="w1gD", align_bytes=64),
+            D: reused.tile([P, H], BF16, name="w1gD", align_bytes=64, offset=2048),
+            B: held.tile([P, H], BF16, name="w1gB", align_bytes=64),
         }
         turn(scopy, A, 0, 2)
         turn(scopy, C, 0, 2)
         turn(vcopy, A, 2, 4)
         turn(scopy, C, 2, 4)
-        turn(vcopy, B, 0, 4)
-        turn(scopy, D, 0, 4)
+        turn(vcopy, D, 0, 4)
+        turn(scopy, B, 0, 4)
         w2g = held.tile([P, N * 4], BF16, name="w2g", align_bytes=64)
         scopy(w2g[:].rearrange("p (n i j) -> p n j i", i=4, j=4), w2raw[:].rearrange("p j (n i) -> p n j i", i=4))
-        for t in (A, C, B):
+        for t in (A, C, D):
             quantise(w1q[t][:], w1s[t][:], w1g[t][:])
         layer1("h0", A, [0, 128])
         layer1("h1", C, [0, 128])
         scatter(acopy, A, 0, 128)
         scatter(acopy, C, 0, 128)
-        quantise(w1q[D][:], w1s[D][:], w1g[D][:])
+        quantise(w1q[B][:], w1s[B][:], w1g[B][:])
         layer1("h2", A, [128, 256, S])
         scatter(acopy, A, 128, S)
-        layer1("h3", B, [0, S])
-        layer1("h5", D, [0, S])
+        layer1("h3", D, [0, S])
         layer1("h6", C, [128, 256, S])
-        scatter(vcopy, B, 0, 160)
-        scatter(vcopy, D, 0, S)
-        scatter(acopy, C, 128, S)
-        scatter(acopy, B, 160, S)
+        layer1("h5", B, [0, S])
         w2q = reused.tile([P, N], U32, name="w2q", align_bytes=64, offset=6144)
 
         zp = reused.tile([P, 2, V, 2], BF16, name="zp", align_bytes=64, offset=8192 - 256)
@@ -156,13 +152,16 @@ def tile_picked_voxel_relu_e_kernel(tc, xT, w1, w2, gate, offs, pos1, out):
             )
             return zg
 
-        rnd(vcopy, A, 0, V)
+        scatter(vcopy, D, 0, 384)
+        rnd(vcopy, A, 512, V)
+        scatter(vcopy, B, 0, 160)
+        rnd(vcopy, A, 0, 512)
+        scatter(acopy, C, 128, S)
+        scatter(acopy, B, 160, S)
+        scatter(vcopy, D, 384, S)
         quantise(w2q[:], w2s[:], w2g[:])
-        zp_d = zp[:, 1].rearrange("p (b c) e -> p b c e", c=256)
-        z_d = z[D][:].rearrange("p (b c) -> p b c", c=256)
-        vcopy(zp_d[:, :, 1:256, 0], z_d[:, :, 1:256])
-        vcopy(zp_d[:, :, 0, :], z_d[:, :, 0:1].to_broadcast([P, 4, 2]))
         rnd(vcopy, C, 0, V)
+        rnd(vcopy, D, 0, V)
 
         res = [held.tile([P, 256], F32, name=f"res{i}") for i in range(4)]
 

from contextlib import ExitStack

import concourse.mybir as mybir

K, T, S, V, H, N = 512, 1024, 512, 1024, 512, 128
P = 128

F32 = mybir.dt.float32
BF16 = mybir.dt.bfloat16
U32 = mybir.dt.uint32
U16 = mybir.dt.uint16
U8 = mybir.dt.uint8
FP8X4 = mybir.dt.float8_e4m3fn_x4
COPY = mybir.ActivationFunctionType.Copy
MULT = mybir.AluOpType.mult
MAX = mybir.AluOpType.max

FLOPS = 2 * H * K * S + 2 * N * H * V


def tile_picked_voxel_relu_e_kernel(tc, xT, w1, w2, gate, offs, pos1, out):
    nc = tc.nc
    vcopy, scopy = nc.vector.tensor_copy, nc.scalar.copy

    def acopy(dst, src):
        nc.scalar.activation(dst, src, COPY)

    with ExitStack() as ctx:
        held = ctx.enter_context(tc.tile_pool(name="held", bufs=1))
        reused = ctx.enter_context(tc.tile_pool(name="reused", bufs=1))
        psum = ctx.enter_context(tc.psum_pool(name="psum", bufs=1))

        points = held.tile([P, S // 16], U16, name="points")
        cells = held.tile([P, S // 16], U16, name="cells")
        gates = reused.tile([P, S], F32, name="gates", align_bytes=64, offset=6144)
        w2raw = held.tile([P, 4, N], F32, name="w2raw", align_bytes=64)
        xv = xT.rearrange("(p j) w -> p j w", j=4)
        wv = w1.rearrange("(p j) w -> p j w", j=4)

        xraw = [held.tile([P, T], F32, name=f"xraw{j}") for j in range(4)]
        w1raw = held.tile([P, 4, H], F32, name="w1raw")
        nc.sync.dma_start(xraw[0][:], xv[:, 0, :])
        nc.sync.dma_start(points[:], offs)
        for j in range(1, 4):
            nc.sync.dma_start(xraw[j][:], xv[:, j, :])
        for b in range(2):
            nc.sync.dma_start(w1raw[:, 2 * b : 2 * b + 2, :], wv[:, 2 * b : 2 * b + 2, :])
        w2v = w2.rearrange("(q t i) n -> i q t n", t=4, i=2)
        for i in range(2):
            nc.sync.dma_start(w2raw[i:P:2], w2v[i])
        nc.sync.dma_start(gates[:], gate)
        nc.sync.dma_start(cells[:], pos1)

        A, B, C, D = 0, 1, 2, 3
        z = [held.tile([P, V], F32, name=f"z{t}") for t in range(4)]
        nc.gpsimd.memset(z[C][:], 0.0)
        acopy(z[A][:], z[C][:])
        nc.gpsimd.memset(z[B][:], 0.0)
        nc.gpsimd.memset(z[D][:], 0.0)

        SH = S // 2
        xg = reused.tile([P, S * 4], BF16, name="xg", align_bytes=64, offset=0)
        xslots = xg[:].rearrange("p (n j) -> p n j", j=4)
        xrows = [held.tile([P, 2, SH], BF16, name=f"xrows{u}") for u in range(2)]
        xq = held.tile([P, S], U32, name="xq", align_bytes=64)
        xs = held.tile([P, S], U8, name="xs", align_bytes=64)
        w1q = [held.tile([P, 128], U32, name=f"w1q{t}", align_bytes=64) for t in range(4)]
        w1s = [held.tile([P, 128], U8, name=f"w1s{t}", align_bytes=64) for t in range(4)]
        w2s = held.tile([P, N], U8, name="w2s", align_bytes=64)
        hg = {t: held.tile([P, S], F32, name=f"hg{t}", align_bytes=64) for t in range(4)}
        zq = held.tile([P, V], U32, name="zq", align_bytes=64)
        zs = held.tile([P, V], U8, name="zs", align_bytes=64)

        def quantise(codes, scales, grouped):
            nc.vector.quantize_mx(out=codes.bitcast(FP8X4), scales=scales, in_=grouped)

        def pick(j):
            vcopy(xslots[:, 0:SH, j], xraw[j][:].indirect(points[:, 0 : SH // 16]))
            acopy(xrows[j // 2][:, j % 2, :], xraw[j][:].indirect(points[:, SH // 16 : S // 16]))

        def weave(copy, u, n0, n1):
            copy(xslots[:, n0:n1, 2 * u : 2 * u + 2], xrows[u][:].rearrange("p j n -> p n j")[:, n0 - SH : n1 - SH])

        def turn(copy, t, j0, j1):
            copy(
                w1g[t][:].rearrange("p (q i j) -> p q j i", i=2, j=4)[:, :, j0:j1],
                w1raw[:].rearrange("p j (q t i) -> p t q j i", t=4, i=2)[:, t, :, j0:j1],
            )

        def scatter(copy, t, n0, n1):
            copy(z[t][:].indirect(cells[:, n0 // 16 : n1 // 16]), hg[t][:, n0:n1])

        def layer1(bank, t, edges):
            acc = psum.tile([P, edges[-1] - edges[0]], F32, name=f"h{t}_{edges[0]}", tag=bank)
            for n0, n1 in zip(edges, edges[1:]):
                nc.tensor.matmul_mx(
                    out=acc[:, n0 - edges[0] : n1 - edges[0]], lhsT=w1q[t][:].bitcast(FP8X4),
                    lhsT_scale=w1s[t][:], rhs=xq[:, n0:n1].bitcast(FP8X4), rhs_scale=xs[:, n0:n1],
                    start=True, stop=True,
                )
            nc.vector.scalar_tensor_tensor(
                hg[t][:, edges[0] : edges[-1]], acc[:], 0.0, gates[:, edges[0] : edges[-1]], MAX, MULT
            )

        pick(0)
        pick(1)
        weave(vcopy, 0, SH, S)
        pick(2)
        pick(3)
        weave(vcopy, 1, SH, 384)
        weave(vcopy, 1, 384, S)
        for n0, n1 in ((0, 384), (384, S)):
            quantise(xq[:, n0:n1], xs[:, n0:n1], xg[:, 4 * n0 : 4 * n1])
        w1g = {
            A: held.tile([P, H], BF16, name="w1gA", align_bytes=64),
            C: held.tile([P, H], BF16, name="w1gC", align_bytes=64),
            D: reused.tile([P, H], BF16, name="w1gD", align_bytes=64, offset=2048),
            B: held.tile([P, H], BF16, name="w1gB", align_bytes=64),
        }
        turn(scopy, A, 0, 2)
        turn(scopy, C, 0, 2)
        turn(vcopy, A, 2, 4)
        turn(scopy, C, 2, 4)
        turn(vcopy, D, 0, 4)
        turn(scopy, B, 0, 4)
        w2g = held.tile([P, N * 4], BF16, name="w2g", align_bytes=64)
        scopy(w2g[:].rearrange("p (n i j) -> p n j i", i=4, j=4), w2raw[:].rearrange("p j (n i) -> p n j i", i=4))
        for t in (A, C, D):
            quantise(w1q[t][:], w1s[t][:], w1g[t][:])
        layer1("h0", A, [0, 128])
        layer1("h1", C, [0, 128])
        scatter(acopy, A, 0, 128)
        scatter(acopy, C, 0, 128)
        quantise(w1q[B][:], w1s[B][:], w1g[B][:])
        layer1("h2", A, [128, 256, S])
        scatter(acopy, A, 128, S)
        layer1("h3", D, [0, S])
        layer1("h6", C, [128, 256, S])
        layer1("h5", B, [0, S])
        w2q = reused.tile([P, N], U32, name="w2q", align_bytes=64, offset=6144)

        zp = reused.tile([P, 2, V, 2], BF16, name="zp", align_bytes=64, offset=8192 - 256)

        def rnd(copy, t, c0, c1):
            copy(zp[:, t // 2, c0:c1, t % 2], z[t][:, c0:c1])

        def join(copy, c0, c1):
            zg = held.tile([P, (c1 - c0) * 4], BF16, name=f"zg{c0}", align_bytes=64)
            copy(
                zg[:].bitcast(U32).rearrange("p (c u) -> p c u", u=2),
                zp[:].rearrange("p u c e -> p (u c e)").bitcast(U32).rearrange("p (u c) -> p c u", u=2)[:, c0:c1],
            )
            return zg

        scatter(vcopy, D, 0, 384)
        rnd(vcopy, A, 512, V)
        scatter(vcopy, B, 0, 160)
        rnd(vcopy, A, 0, 512)
        scatter(acopy, C, 128, S)
        scatter(acopy, B, 160, S)
        scatter(vcopy, D, 384, S)
        quantise(w2q[:], w2s[:], w2g[:])
        rnd(vcopy, C, 0, V)
        rnd(vcopy, D, 0, V)

        res = [held.tile([P, 256], F32, name=f"res{i}") for i in range(4)]

        banks = {}

        def layer2(c0, c1, zg):
            quantise(zq[:, c0:c1], zs[:, c0:c1], zg[:])
            for c in range(c0, c1, 128):
                banks[c] = psum.tile([P, 128], F32, name=f"o{c}", tag=f"h{c // 128}")
                nc.tensor.matmul_mx(
                    out=banks[c][:], lhsT=w2q[:].bitcast(FP8X4), lhsT_scale=w2s[:],
                    rhs=zq[:, c : c + 128].bitcast(FP8X4), rhs_scale=zs[:, c : c + 128], start=True, stop=True,
                )

        rnd(vcopy, B, 0, 256)
        rnd(vcopy, B, 256, 512)
        rnd(scopy, B, 512, 768)
        rnd(scopy, B, 768, V)
        g2 = join(scopy, 512, 768)
        g3 = join(scopy, 768, 896)
        g4 = join(scopy, 896, V)
        g0 = join(vcopy, 0, 256)
        g1 = join(vcopy, 256, 512)
        layer2(0, 256, g0)
        layer2(256, 512, g1)
        layer2(512, 768, g2)
        layer2(768, 896, g3)
        layer2(896, V, g4)
        for c in range(0, V, 128):
            copy = vcopy if c >= 384 and c % 256 else scopy
            copy(res[c // 256][:, c % 256 : c % 256 + 128], banks[c][:])
            if c < 256:
                nc.sync.dma_start(out[:, c : c + 128], res[0][:, c : c + 128])
            elif c % 256:
                nc.sync.dma_start(out[:, c - 128 : c + 128], res[c // 256][:])
